import numpy as np
import ml_dtypes


def mxq(x, axis, fmt="e4m3"):
    dtype, down = {"e4m3": (ml_dtypes.float8_e4m3fn, 7), "e5m2": (ml_dtypes.float8_e5m2, 14)}[fmt]
    v = np.moveaxis(np.asarray(x, np.float32).astype(ml_dtypes.bfloat16).astype(np.float64), axis, -1)
    blocks = v.reshape(v.shape[:-1] + (-1, 32))
    amax = np.abs(blocks).max(-1, keepdims=True)
    byte = np.maximum(np.where(amax > 0, np.frexp(amax)[1] - 1 + 127, 0) - down, 1)
    scale = np.exp2(byte - 127.0)
    codes = (blocks / scale).astype(np.float32).astype(dtype).astype(np.float64)
    return np.moveaxis((codes * scale).reshape(v.shape), -1, axis)


WIDE = False


def mx_kscale(k):
    if not WIDE:
        return np.ones(k)
    levels = np.array([10, -10, 5, -5, 0])
    if k % 512:
        return np.exp2(np.random.permutation(np.resize(levels, k // 32))).repeat(32)
    a = np.empty((k // 512, 16))
    for p in range(k // 512):
        a[p, :8] = np.random.permutation(np.resize(levels, 8))
        for g in range(8):
            far = levels[np.abs(levels - a[p, g]) >= 10]
            a[p, g + 8] = far[np.random.randint(len(far))]
    return np.exp2(a.ravel()).repeat(32)


def f64(x):
    return np.asarray(x).astype(np.float64)


def striped(idx):
    return np.tile(idx.reshape(-1, 16).T, (8, 1)).astype(np.uint16)


def unstriped(offs):
    return offs[:16].T.reshape(-1).astype(np.int64)


E2M1 = np.array([0.0, 0.5, 1.0, 1.5, 2.0, 3.0, 4.0, 6.0, -0.0, -0.5, -1.0, -1.5, -2.0, -3.0, -4.0, -6.0])


def pack_weight(w, fmt):
    k, n = w.shape
    w = f64(np.asarray(w, np.float32).astype(ml_dtypes.bfloat16)).reshape(k // 32, 32, n)
    amax = np.abs(w).max(1)
    if fmt == "e4m3":
        byte = np.frexp(amax)[1] - 1 + 127 - 7
    else:
        mant, ex = np.frexp(amax / 6.0)
        byte = np.where(mant > 0.5, ex, ex - 1) + 127
    byte = np.clip(np.where(amax > 0, byte, 1), 1, 254)
    scaled = (w * np.exp2(127.0 - byte)[:, None, :]).reshape(k, n).astype(np.float32)
    by_word = np.ascontiguousarray(scaled.reshape(k // 512, 128, 4, n).transpose(0, 1, 3, 2))
    if fmt == "e4m3":
        words = by_word.astype(ml_dtypes.float8_e4m3fn).view(np.uint8)
    else:
        c = by_word.astype(ml_dtypes.float4_e2m1fn).view(np.uint8) & 0xF
        words = (c[..., 0::2] | (c[..., 1::2] << 4)).reshape(k // 512, 128, 2 * n)
    return np.ascontiguousarray(words), np.ascontiguousarray(byte.astype(np.uint8).reshape(k // 512, 16, n))


def unpack_weight(words, scales, fmt):
    g, _, n = scales.shape
    words = np.ascontiguousarray(words).reshape(g, 128, n, -1)
    if fmt == "e4m3":
        vals = words.view(ml_dtypes.float8_e4m3fn).astype(np.float64)
    else:
        nib = np.empty((g, 128, n, 4), np.uint8)
        nib[..., 0::2] = words & 0xF
        nib[..., 1::2] = words >> 4
        vals = E2M1[nib]
    vals = vals * np.repeat(np.exp2(scales.astype(np.float64) - 127.0), 8, axis=1)[..., None]
    return vals.transpose(0, 1, 3, 2).reshape(g * 512, n)


K, T, E, C, N = 1024, 2048, 8, 128, 384


def by_expert(wq, xq):
    return np.concatenate([wq[e].T @ xq[:, e * C:(e + 1) * C] for e in range(E)], axis=1)


def setup_inputs():
    n = np.random.standard_normal
    s = mx_kscale(K)[:, None]
    x = pack_weight(n((K, T)) * s, "e4m3")
    return {
        "x_words": x[0],
        "x_scales": x[1],
        "xr": n((N, T)).astype(np.float32),
        "w": (n((E, K, N)) / np.sqrt(K) / s[None]).astype(np.float32),
        "gate": np.tile(np.random.uniform(0.2, 1.0, E * C), (N, 1)).astype(np.float32),
        "offs": striped(np.random.permutation(T)[:E * C]),
    }


def reference(x_words, x_scales, xr, w, gate, offs):
    idx = unstriped(offs)
    xq = unpack_weight(x_words, x_scales, "e4m3")[:, idx]
    y = by_expert(mxq(f64(w), 1, "e4m3"), xq)
    out = f64(xr).copy()
    out[:, idx] += f64(gate) * y
    return out

@@ -1,0 +1,133 @@
+from contextlib import ExitStack
+
+import concourse.mybir as mybir
+
+K, T, E, C, N = 1024, 2048, 8, 128, 384
+FLOPS = 2 * K * N * E * C
+
+F32 = mybir.dt.float32
+BF16 = mybir.dt.bfloat16
+I32 = mybir.dt.int32
+U32 = mybir.dt.uint32
+U16 = mybir.dt.uint16
+U8 = mybir.dt.uint8
+FP8X4 = mybir.dt.float8_e4m3fn_x4
+MULT = mybir.AluOpType.mult
+ADD = mybir.AluOpType.add
+
+P = 128
+PACK = 4
+K_PASS = P * PACK
+PASSES = K // K_PASS
+BLOCKS = N // P
+SLOTS = E * C
+PAIR = 2 * C
+LIST_ROWS = 16
+ON_VECTOR = ((0, 1), (1, 1), (2, 1), (4, 1))
+
+
+def tile_moe_res_lin_none_kernel(tc, x_words, x_scales, xr, w, gate, offs, out):
+    nc = tc.nc
+    with ExitStack() as ctx:
+        keep = ctx.enter_context(tc.tile_pool(name="keep", bufs=1))
+        raw_pool = ctx.enter_context(tc.tile_pool(name="raw", bufs=16))
+        ring = ctx.enter_context(tc.tile_pool(name="ring", bufs=4))
+        psum = ctx.enter_context(tc.psum_pool(name="psum", bufs=2))
+
+        offsets = keep.tile([P, SLOTS // LIST_ROWS], U16, name="offsets")
+        landed_scales = keep.tile([P, T], U8, name="landed_scales")
+        token_scales = keep.tile([P, T], U8, name="token_scales")
+        token_words = [keep.tile([P, T], I32, name="token_words%d" % o) for o in range(PASSES)]
+        slot_words = [keep.tile([P, SLOTS], U32, name="slot_words%d" % o, align_bytes=64) for o in range(PASSES)]
+        slot_scales = keep.tile([P, SLOTS], U8, name="slot_scales", align_bytes=64)
+        gates = [keep.tile([P, PAIR], F32, name="gate%d" % q) for q in range(E // 2)]
+        routed = [keep.tile([P, T], F32, name="routed%d" % b) for b in range(BLOCKS)]
+        resid = [keep.tile([P, T], F32, name="resid%d" % b) for b in range(BLOCKS)]
+        sums = [keep.tile([P, BLOCKS, PAIR], F32, name="sums%d" % q) for q in range(E // 2)]
+
+        raw = {}
+
+        def load_w(e, o):
+            raw[e, o] = raw_pool.tile([P, PACK, N], F32, name="raw")
+            nc.sync.dma_start(out=raw[e, o][:], in_=w[e, o * K_PASS:(o + 1) * K_PASS, :].rearrange("(p t) n -> p t n", t=PACK))
+
+        def load_x(o):
+            nc.sync.dma_start(out=token_words[o][:], in_=x_words[o].rearrange("p t r -> p (t r)").bitcast(I32))
+
+        nc.vector.memset(token_scales[:].bitcast(I32), 0)
+        nc.sync.dma_start(offsets[:], offs)
+        for q in range(4):
+            rows = slice(32 * q, 32 * q + 4 * PASSES)
+            nc.sync.dma_start(out=landed_scales[rows, :].bitcast(I32), in_=x_scales[:, 4 * q:4 * q + 4, :].bitcast(I32))
+            nc.vector.tensor_copy(token_scales[rows, :].bitcast(I32), landed_scales[rows, :].bitcast(I32))
+        load_x(0)
+        load_x(1)
+        for e in range(E):
+            for o in range(PASSES):
+                load_w(e, o)
+            if e % 2 == 1:
+                q = e // 2
+                nc.sync.dma_start(out=gates[q][:], in_=gate[0:P, q * PAIR:(q + 1) * PAIR])
+        for b in range(BLOCKS):
+            nc.sync.dma_start(out=resid[b][:], in_=xr[b * P:(b + 1) * P, :])
+        for b in range(BLOCKS):
+            nc.gpsimd.memset(routed[b][:], 0.0)
+
+        nc.vector.tensor_copy(slot_scales[:], token_scales[:].indirect(offsets[:]))
+        nc.vector.tensor_copy(slot_words[0][:], token_words[0][:].bitcast(U32).indirect(offsets[:]))
+        nc.vector.tensor_copy(slot_words[1][:], token_words[1][:].bitcast(U32).indirect(offsets[:]))
+
+        def cast(engine_copy, grouped, e, o, b0, b1):
+            engine_copy(
+                out=grouped[:, b0:b1, o, :].rearrange("p b (c i t) -> p b c t i", i=4, t=PACK),
+                in_=raw[e, o][:, :, b0 * P:b1 * P].rearrange("p t (b c i) -> p b c t i", i=4, b=b1 - b0),
+            )
+
+        def cast_run(grouped, e, o, b0, b1):
+            last = BLOCKS - 1
+            if b1 == BLOCKS and (e, o) in ON_VECTOR:
+                cast(nc.vector.tensor_copy, grouped, e, o, last, BLOCKS)
+                b1 = last
+            if b1 > b0:
+                cast(nc.scalar.copy, grouped, e, o, b0, b1)
+
+        def expert(e, acc):
+            grouped = ring.tile([P, BLOCKS, PASSES, P * PACK], BF16, name="grouped", align_bytes=64)
+            codes = ring.tile([P, BLOCKS * PASSES * P], U32, name="codes", align_bytes=64)
+            scales = ring.tile([P, BLOCKS * PASSES * P], U8, name="scales", align_bytes=64)
+            cast_run(grouped, e, 0, 0, BLOCKS)
+            slots = slice(e * C, (e + 1) * C)
+            place = slice((e % 2) * C, (e % 2 + 1) * C)
+            runs = ((0, 1), (1, 2), (2, 3)) if e % 2 == 1 else ((0, 2), (2, 3))
+            for b0, b1 in runs:
+                cast_run(grouped, e, 1, b0, b1)
+                cols = slice(b0 * PASSES * P, b1 * PASSES * P)
+                nc.vector.quantize_mx(out=codes[:, cols].bitcast(FP8X4), scales=scales[:, cols],
+                                      in_=grouped[:, b0:b1, :, :].rearrange("p b o x -> p (b o x)"))
+                for b in range(b0, b1):
+                    for o in range(PASSES):
+                        cols = slice((b * PASSES + o) * P, (b * PASSES + o + 1) * P)
+                        nc.tensor.matmul_mx(out=acc[b][:, place], lhsT=codes[:, cols].bitcast(FP8X4), lhsT_scale=scales[:, cols],
+                                            rhs=slot_words[o][:, slots].bitcast(FP8X4), rhs_scale=slot_scales[4 * o:P, slots],
+                                            start=(o == 0), stop=(o == PASSES - 1))
+                    if e % 2 == 1:
+                        nc.scalar.copy(out=sums[e // 2][:, b, :], in_=acc[b][:])
+
+        def scatter(q, b):
+            cols = slice(q * PAIR // LIST_ROWS, (q + 1) * PAIR // LIST_ROWS)
+            nc.vector.tensor_tensor(routed[b][:].indirect(offsets[:, cols]), sums[q][:, b, :], gates[q][:], MULT)
+
+        for e in range(E):
+            if e % 2 == 0:
+                acc = [psum.tile([P, PAIR], F32, name="acc%d" % b) for b in range(BLOCKS)]
+            expert(e, acc)
+            if e % 2 == 1 and e < E - 1:
+                for b in range(BLOCKS):
+                    scatter(e // 2, b)
+        for b in range(BLOCKS):
+            scatter(E // 2 - 1, b)
+            cuts = (0, T // 2, T) if b < BLOCKS - 1 else (0, T // 2, 3 * T // 4, T)
+            for lo, hi in zip(cuts, cuts[1:]):
+                cols = slice(lo, hi)
+                nc.vector.tensor_tensor(resid[b][:, cols], resid[b][:, cols], routed[b][:, cols], ADD)
+                nc.sync.dma_start(out=out[b * P:(b + 1) * P, cols], in_=resid[b][:, cols])

@@ -23,7 +23,7 @@ BLOCKS = N // P
 SLOTS = E * C
 PAIR = 2 * C
 LIST_ROWS = 16
-ON_VECTOR = ((0, 1), (1, 1), (2, 1), (4, 1))
+ON_VECTOR = ((0, 1, 2), (1, 0, 2), (1, 1, 0), (2, 0, 2), (4, 0, 2), (6, 0, 2))
 
 
 def tile_moe_res_lin_none_kernel(tc, x_words, x_scales, xr, w, gate, offs, out):
@@ -61,17 +61,20 @@ def tile_moe_res_lin_none_kernel(tc, x_words, x_scales, xr, w, gate, offs, out):
             nc.sync.dma_start(out=landed_scales[rows, :].bitcast(I32), in_=x_scales[:, 4 * q:4 * q + 4, :].bitcast(I32))
             nc.vector.tensor_copy(token_scales[rows, :].bitcast(I32), landed_scales[rows, :].bitcast(I32))
         load_x(0)
+        load_w(0, 0)
         load_x(1)
         for e in range(E):
             for o in range(PASSES):
-                load_w(e, o)
+                if (e, o) not in raw:
+                    load_w(e, o)
             if e % 2 == 1:
                 q = e // 2
                 nc.sync.dma_start(out=gates[q][:], in_=gate[0:P, q * PAIR:(q + 1) * PAIR])
         for b in range(BLOCKS):
             nc.sync.dma_start(out=resid[b][:], in_=xr[b * P:(b + 1) * P, :])
-        for b in range(BLOCKS):
-            nc.gpsimd.memset(routed[b][:], 0.0)
+        nc.vector.memset(routed[0][:], 0.0)
+        for b in range(1, BLOCKS):
+            nc.scalar.copy(out=routed[b][:], in_=routed[0][:])
 
         nc.vector.tensor_copy(slot_scales[:], token_scales[:].indirect(offsets[:]))
         nc.vector.tensor_copy(slot_words[0][:], token_words[0][:].bitcast(U32).indirect(offsets[:]))
@@ -84,12 +87,12 @@ def tile_moe_res_lin_none_kernel(tc, x_words, x_scales, xr, w, gate, offs, out):
             )
 
         def cast_run(grouped, e, o, b0, b1):
-            last = BLOCKS - 1
-            if b1 == BLOCKS and (e, o) in ON_VECTOR:
-                cast(nc.vector.tensor_copy, grouped, e, o, last, BLOCKS)
-                b1 = last
-            if b1 > b0:
-                cast(nc.scalar.copy, grouped, e, o, b0, b1)
+            rest = [b for b in range(b0, b1) if (e, o, b) not in ON_VECTOR]
+            for b in range(b0, b1):
+                if b not in rest:
+                    cast(nc.vector.tensor_copy, grouped, e, o, b, b + 1)
+            if rest:
+                cast(nc.scalar.copy, grouped, e, o, rest[0], rest[-1] + 1)
 
         def expert(e, acc):
             grouped = ring.tile([P, BLOCKS, PASSES, P * PACK], BF16, name="grouped", align_bytes=64)

@@ -20,19 +20,29 @@ PACK = 4
 K_PASS = P * PACK
 PASSES = K // K_PASS
 BLOCKS = N // P
+LAST_BLOCK = BLOCKS - 1
 SLOTS = E * C
+PAIRS = E // 2
 PAIR = 2 * C
 LIST_ROWS = 16
-ON_VECTOR = ((0, 1, 2), (1, 0, 2), (1, 1, 0), (2, 0, 2), (4, 0, 2), (6, 0, 2))
+QUADRANT = 32
+SCALE_ROWS = 4
+RUN = 4
+CODES_DEPTH = 4
+SUMS_DEPTH = 2
+
+
+def rounded_on_vector(e, o, b):
+    return b == LAST_BLOCK and (e == 1 or (e > 1 and e % 2 == 0 and o == 0))
 
 
 def tile_moe_res_lin_none_kernel(tc, x_words, x_scales, xr, w, gate, offs, out):
     nc = tc.nc
     with ExitStack() as ctx:
         keep = ctx.enter_context(tc.tile_pool(name="keep", bufs=1))
-        raw_pool = ctx.enter_context(tc.tile_pool(name="raw", bufs=16))
-        ring = ctx.enter_context(tc.tile_pool(name="ring", bufs=4))
-        psum = ctx.enter_context(tc.psum_pool(name="psum", bufs=2))
+        raw_pool = ctx.enter_context(tc.tile_pool(name="raw", bufs=E * PASSES))
+        ring = ctx.enter_context(tc.tile_pool(name="ring", bufs=CODES_DEPTH))
+        psum = ctx.enter_context(tc.psum_pool(name="psum", bufs=SUMS_DEPTH))
 
         offsets = keep.tile([P, SLOTS // LIST_ROWS], U16, name="offsets")
         landed_scales = keep.tile([P, T], U8, name="landed_scales")
@@ -40,10 +50,10 @@ def tile_moe_res_lin_none_kernel(tc, x_words, x_scales, xr, w, gate, offs, out):
         token_words = [keep.tile([P, T], I32, name="token_words%d" % o) for o in range(PASSES)]
         slot_words = [keep.tile([P, SLOTS], U32, name="slot_words%d" % o, align_bytes=64) for o in range(PASSES)]
         slot_scales = keep.tile([P, SLOTS], U8, name="slot_scales", align_bytes=64)
-        gates = [keep.tile([P, PAIR], F32, name="gate%d" % q) for q in range(E // 2)]
+        gates = [keep.tile([P, PAIR], F32, name="gate%d" % q) for q in range(PAIRS)]
         routed = [keep.tile([P, T], F32, name="routed%d" % b) for b in range(BLOCKS)]
         resid = [keep.tile([P, T], F32, name="resid%d" % b) for b in range(BLOCKS)]
-        sums = [keep.tile([P, BLOCKS, PAIR], F32, name="sums%d" % q) for q in range(E // 2)]
+        sums = [keep.tile([P, BLOCKS, PAIR], F32, name="sums%d" % q) for q in range(PAIRS)]
 
         raw = {}
 
@@ -56,10 +66,12 @@ def tile_moe_res_lin_none_kernel(tc, x_words, x_scales, xr, w, gate, offs, out):
 
         nc.vector.memset(token_scales[:].bitcast(I32), 0)
         nc.sync.dma_start(offsets[:], offs)
-        for q in range(4):
-            rows = slice(32 * q, 32 * q + 4 * PASSES)
-            nc.sync.dma_start(out=landed_scales[rows, :].bitcast(I32), in_=x_scales[:, 4 * q:4 * q + 4, :].bitcast(I32))
+        for quad in range(P // QUADRANT):
+            rows = slice(QUADRANT * quad, QUADRANT * quad + SCALE_ROWS * PASSES)
+            nc.sync.dma_start(out=landed_scales[rows, :].bitcast(I32),
+                              in_=x_scales[:, SCALE_ROWS * quad:SCALE_ROWS * (quad + 1), :].bitcast(I32))
             nc.vector.tensor_copy(token_scales[rows, :].bitcast(I32), landed_scales[rows, :].bitcast(I32))
+
         load_x(0)
         load_w(0, 0)
         load_x(1)
@@ -72,53 +84,55 @@ def tile_moe_res_lin_none_kernel(tc, x_words, x_scales, xr, w, gate, offs, out):
                 nc.sync.dma_start(out=gates[q][:], in_=gate[0:P, q * PAIR:(q + 1) * PAIR])
         for b in range(BLOCKS):
             nc.sync.dma_start(out=resid[b][:], in_=xr[b * P:(b + 1) * P, :])
+
         nc.vector.memset(routed[0][:], 0.0)
         for b in range(1, BLOCKS):
             nc.scalar.copy(out=routed[b][:], in_=routed[0][:])
 
         nc.vector.tensor_copy(slot_scales[:], token_scales[:].indirect(offsets[:]))
-        nc.vector.tensor_copy(slot_words[0][:], token_words[0][:].bitcast(U32).indirect(offsets[:]))
-        nc.vector.tensor_copy(slot_words[1][:], token_words[1][:].bitcast(U32).indirect(offsets[:]))
+        for o in range(PASSES):
+            nc.vector.tensor_copy(slot_words[o][:], token_words[o][:].bitcast(U32).indirect(offsets[:]))
 
-        def cast(engine_copy, grouped, e, o, b0, b1):
+        def interleave(engine_copy, grouped, e, o, b0, b1):
             engine_copy(
-                out=grouped[:, b0:b1, o, :].rearrange("p b (c i t) -> p b c t i", i=4, t=PACK),
-                in_=raw[e, o][:, :, b0 * P:b1 * P].rearrange("p t (b c i) -> p b c t i", i=4, b=b1 - b0),
+                out=grouped[:, b0:b1, o, :].rearrange("p b (c i t) -> p b c t i", i=RUN, t=PACK),
+                in_=raw[e, o][:, :, b0 * P:b1 * P].rearrange("p t (b c i) -> p b c t i", i=RUN, b=b1 - b0),
             )
 
-        def cast_run(grouped, e, o, b0, b1):
-            rest = [b for b in range(b0, b1) if (e, o, b) not in ON_VECTOR]
-            for b in range(b0, b1):
-                if b not in rest:
-                    cast(nc.vector.tensor_copy, grouped, e, o, b, b + 1)
-            if rest:
-                cast(nc.scalar.copy, grouped, e, o, rest[0], rest[-1] + 1)
+        def round_blocks(grouped, e, o, b0, b1):
+            if rounded_on_vector(e, o, b1 - 1):
+                interleave(nc.vector.tensor_copy, grouped, e, o, b1 - 1, b1)
+                b1 = b1 - 1
+            if b1 > b0:
+                interleave(nc.scalar.copy, grouped, e, o, b0, b1)
 
         def expert(e, acc):
             grouped = ring.tile([P, BLOCKS, PASSES, P * PACK], BF16, name="grouped", align_bytes=64)
             codes = ring.tile([P, BLOCKS * PASSES * P], U32, name="codes", align_bytes=64)
             scales = ring.tile([P, BLOCKS * PASSES * P], U8, name="scales", align_bytes=64)
-            cast_run(grouped, e, 0, 0, BLOCKS)
+            round_blocks(grouped, e, 0, 0, BLOCKS)
             slots = slice(e * C, (e + 1) * C)
             place = slice((e % 2) * C, (e % 2 + 1) * C)
             runs = ((0, 1), (1, 2), (2, 3)) if e % 2 == 1 else ((0, 2), (2, 3))
             for b0, b1 in runs:
-                cast_run(grouped, e, 1, b0, b1)
-                cols = slice(b0 * PASSES * P, b1 * PASSES * P)
-                nc.vector.quantize_mx(out=codes[:, cols].bitcast(FP8X4), scales=scales[:, cols],
+                round_blocks(grouped, e, 1, b0, b1)
+                run_cols = slice(b0 * PASSES * P, b1 * PASSES * P)
+                nc.vector.quantize_mx(out=codes[:, run_cols].bitcast(FP8X4), scales=scales[:, run_cols],
                                       in_=grouped[:, b0:b1, :, :].rearrange("p b o x -> p (b o x)"))
                 for b in range(b0, b1):
                     for o in range(PASSES):
-                        cols = slice((b * PASSES + o) * P, (b * PASSES + o + 1) * P)
-                        nc.tensor.matmul_mx(out=acc[b][:, place], lhsT=codes[:, cols].bitcast(FP8X4), lhsT_scale=scales[:, cols],
-                                            rhs=slot_words[o][:, slots].bitcast(FP8X4), rhs_scale=slot_scales[4 * o:P, slots],
+                        w_cols = slice((b * PASSES + o) * P, (b * PASSES + o + 1) * P)
+                        nc.tensor.matmul_mx(out=acc[b][:, place],
+                                            lhsT=codes[:, w_cols].bitcast(FP8X4), lhsT_scale=scales[:, w_cols],
+                                            rhs=slot_words[o][:, slots].bitcast(FP8X4),
+                                            rhs_scale=slot_scales[SCALE_ROWS * o:P, slots],
                                             start=(o == 0), stop=(o == PASSES - 1))
-                    if e % 2 == 1:
+                    if e % 2 == 1 and (e, b) != (E - 1, LAST_BLOCK):
                         nc.scalar.copy(out=sums[e // 2][:, b, :], in_=acc[b][:])
 
-        def scatter(q, b):
-            cols = slice(q * PAIR // LIST_ROWS, (q + 1) * PAIR // LIST_ROWS)
-            nc.vector.tensor_tensor(routed[b][:].indirect(offsets[:, cols]), sums[q][:, b, :], gates[q][:], MULT)
+        def scatter(q, b, values):
+            entries = slice(q * PAIR // LIST_ROWS, (q + 1) * PAIR // LIST_ROWS)
+            nc.vector.tensor_tensor(routed[b][:].indirect(offsets[:, entries]), values, gates[q][:], MULT)
 
         for e in range(E):
             if e % 2 == 0:
@@ -126,11 +140,21 @@ def tile_moe_res_lin_none_kernel(tc, x_words, x_scales, xr, w, gate, offs, out):
             expert(e, acc)
             if e % 2 == 1 and e < E - 1:
                 for b in range(BLOCKS):
-                    scatter(e // 2, b)
-        for b in range(BLOCKS):
-            scatter(E // 2 - 1, b)
-            cuts = (0, T // 2, T) if b < BLOCKS - 1 else (0, T // 2, 3 * T // 4, T)
+                    scatter(e // 2, b, sums[e // 2][:, b, :])
+
+        def add_and_store(b, cuts):
             for lo, hi in zip(cuts, cuts[1:]):
-                cols = slice(lo, hi)
-                nc.vector.tensor_tensor(resid[b][:, cols], resid[b][:, cols], routed[b][:, cols], ADD)
-                nc.sync.dma_start(out=out[b * P:(b + 1) * P, cols], in_=resid[b][:, cols])
+                tokens = slice(lo, hi)
+                nc.vector.tensor_tensor(resid[b][:, tokens], resid[b][:, tokens], routed[b][:, tokens], ADD)
+                nc.sync.dma_start(out=out[b * P:(b + 1) * P, tokens], in_=resid[b][:, tokens])
+
+        last = PAIRS - 1
+        scatter(last, 0, sums[last][:, 0, :])
+        add_and_store(0, (0, T // 2, T))
+        scatter(last, 1, sums[last][:, 1, :])
+        add_and_store(1, (0, T // 2))
+        spare = routed[0][:, T - PAIR:T]
+        nc.scalar.copy(out=spare, in_=acc[LAST_BLOCK][:])
+        scatter(last, LAST_BLOCK, spare)
+        add_and_store(1, (T // 2, T))
+        add_and_store(LAST_BLOCK, (0, T // 2, 3 * T // 4, T))

@@ -1,6 +1,7 @@
 from contextlib import ExitStack
 
 import concourse.mybir as mybir
+from concourse.masks import make_identity
 
 K, T, E, C, N = 1024, 2048, 8, 128, 384
 FLOPS = 2 * K * N * E * C
@@ -29,11 +30,13 @@ QUADRANT = 32
 SCALE_ROWS = 4
 RUN = 4
 CODES_DEPTH = 4
-SUMS_DEPTH = 2
+CHUNKS = T // 512
+GATE_ROW = SLOTS // P
+BANK = 512
 
 
 def rounded_on_vector(e, o, b):
-    return b == LAST_BLOCK and (e == 1 or (e > 1 and e % 2 == 0 and o == 0))
+    return b == LAST_BLOCK and e == 1
 
 
 def tile_moe_res_lin_none_kernel(tc, x_words, x_scales, xr, w, gate, offs, out):
@@ -42,7 +45,7 @@ def tile_moe_res_lin_none_kernel(tc, x_words, x_scales, xr, w, gate, offs, out):
         keep = ctx.enter_context(tc.tile_pool(name="keep", bufs=1))
         raw_pool = ctx.enter_context(tc.tile_pool(name="raw", bufs=E * PASSES))
         ring = ctx.enter_context(tc.tile_pool(name="ring", bufs=CODES_DEPTH))
-        psum = ctx.enter_context(tc.psum_pool(name="psum", bufs=SUMS_DEPTH))
+        psum = ctx.enter_context(tc.psum_pool(name="psum", bufs=1))
 
         offsets = keep.tile([P, SLOTS // LIST_ROWS], U16, name="offsets")
         landed_scales = keep.tile([P, T], U8, name="landed_scales")
@@ -50,7 +53,9 @@ def tile_moe_res_lin_none_kernel(tc, x_words, x_scales, xr, w, gate, offs, out):
         token_words = [keep.tile([P, T], I32, name="token_words%d" % o) for o in range(PASSES)]
         slot_words = [keep.tile([P, SLOTS], U32, name="slot_words%d" % o, align_bytes=64) for o in range(PASSES)]
         slot_scales = keep.tile([P, SLOTS], U8, name="slot_scales", align_bytes=64)
-        gates = [keep.tile([P, PAIR], F32, name="gate%d" % q) for q in range(PAIRS)]
+        gate_row = keep.tile([P, GATE_ROW], F32, name="gate_row")
+        gates = keep.tile([P, SLOTS], F32, name="gates")
+        identity = keep.tile([P, P], F32, name="identity")
         routed = [keep.tile([P, T], F32, name="routed%d" % b) for b in range(BLOCKS)]
         resid = [keep.tile([P, T], F32, name="resid%d" % b) for b in range(BLOCKS)]
         sums = [keep.tile([P, BLOCKS, PAIR], F32, name="sums%d" % q) for q in range(PAIRS)]
@@ -66,6 +71,7 @@ def tile_moe_res_lin_none_kernel(tc, x_words, x_scales, xr, w, gate, offs, out):
 
         nc.vector.memset(token_scales[:].bitcast(I32), 0)
         nc.sync.dma_start(offsets[:], offs)
+        nc.sync.dma_start(out=gate_row[:], in_=gate[0, :].rearrange("(p i) -> p i", i=GATE_ROW))
         for quad in range(P // QUADRANT):
             rows = slice(QUADRANT * quad, QUADRANT * quad + SCALE_ROWS * PASSES)
             nc.sync.dma_start(out=landed_scales[rows, :].bitcast(I32),
@@ -79,15 +85,22 @@ def tile_moe_res_lin_none_kernel(tc, x_words, x_scales, xr, w, gate, offs, out):
             for o in range(PASSES):
                 if (e, o) not in raw:
                     load_w(e, o)
-            if e % 2 == 1:
-                q = e // 2
-                nc.sync.dma_start(out=gates[q][:], in_=gate[0:P, q * PAIR:(q + 1) * PAIR])
         for b in range(BLOCKS):
             nc.sync.dma_start(out=resid[b][:], in_=xr[b * P:(b + 1) * P, :])
 
         nc.vector.memset(routed[0][:], 0.0)
         for b in range(1, BLOCKS):
             nc.scalar.copy(out=routed[b][:], in_=routed[0][:])
+
+        make_identity(nc, identity[:])
+        per_bank = BANK // P
+        for h in range(GATE_ROW // per_bank):
+            spread = psum.tile([P, per_bank, P], F32, name="bank%d" % h)
+            for i in range(per_bank):
+                column = h * per_bank + i
+                nc.tensor.transpose(spread[:, i, :], gate_row[:, column:column + 1].to_broadcast([P, P]), identity[:])
+            nc.scalar.copy(out=gates[:].rearrange("p (s i) -> p s i", i=GATE_ROW)[:, :, h * per_bank:(h + 1) * per_bank],
+                           in_=spread[:].rearrange("p i s -> p s i"))
 
         nc.vector.tensor_copy(slot_scales[:], token_scales[:].indirect(offsets[:]))
         for o in range(PASSES):
@@ -106,41 +119,31 @@ def tile_moe_res_lin_none_kernel(tc, x_words, x_scales, xr, w, gate, offs, out):
             if b1 > b0:
                 interleave(nc.scalar.copy, grouped, e, o, b0, b1)
 
-        def expert(e, acc):
+        def new_expert():
             grouped = ring.tile([P, BLOCKS, PASSES, P * PACK], BF16, name="grouped", align_bytes=64)
             codes = ring.tile([P, BLOCKS * PASSES * P], U32, name="codes", align_bytes=64)
             scales = ring.tile([P, BLOCKS * PASSES * P], U8, name="scales", align_bytes=64)
-            round_blocks(grouped, e, 0, 0, BLOCKS)
+            return grouped, codes, scales
+
+        def multiply(tiles, e, acc, b0, b1):
+            grouped, codes, scales = tiles
             slots = slice(e * C, (e + 1) * C)
             place = slice((e % 2) * C, (e % 2 + 1) * C)
-            runs = ((0, 1), (1, 2), (2, 3)) if e % 2 == 1 else ((0, 2), (2, 3))
-            for b0, b1 in runs:
-                round_blocks(grouped, e, 1, b0, b1)
-                run_cols = slice(b0 * PASSES * P, b1 * PASSES * P)
-                nc.vector.quantize_mx(out=codes[:, run_cols].bitcast(FP8X4), scales=scales[:, run_cols],
-                                      in_=grouped[:, b0:b1, :, :].rearrange("p b o x -> p (b o x)"))
-                for b in range(b0, b1):
-                    for o in range(PASSES):
-                        w_cols = slice((b * PASSES + o) * P, (b * PASSES + o + 1) * P)
-                        nc.tensor.matmul_mx(out=acc[b][:, place],
-                                            lhsT=codes[:, w_cols].bitcast(FP8X4), lhsT_scale=scales[:, w_cols],
-                                            rhs=slot_words[o][:, slots].bitcast(FP8X4),
-                                            rhs_scale=slot_scales[SCALE_ROWS * o:P, slots],
-                                            start=(o == 0), stop=(o == PASSES - 1))
-                    if e % 2 == 1 and (e, b) != (E - 1, LAST_BLOCK):
-                        nc.scalar.copy(out=sums[e // 2][:, b, :], in_=acc[b][:])
+            run_cols = slice(b0 * PASSES * P, b1 * PASSES * P)
+            nc.vector.quantize_mx(out=codes[:, run_cols].bitcast(FP8X4), scales=scales[:, run_cols],
+                                  in_=grouped[:, b0:b1, :, :].rearrange("p b o x -> p (b o x)"))
+            for b in range(b0, b1):
+                for o in range(PASSES):
+                    w_cols = slice((b * PASSES + o) * P, (b * PASSES + o + 1) * P)
+                    nc.tensor.matmul_mx(out=acc[b][:, place],
+                                        lhsT=codes[:, w_cols].bitcast(FP8X4), lhsT_scale=scales[:, w_cols],
+                                        rhs=slot_words[o][:, slots].bitcast(FP8X4),
+                                        rhs_scale=slot_scales[SCALE_ROWS * o:P, slots],
+                                        start=(o == 0), stop=(o == PASSES - 1))
 
         def scatter(q, b, values):
             entries = slice(q * PAIR // LIST_ROWS, (q + 1) * PAIR // LIST_ROWS)
-            nc.vector.tensor_tensor(routed[b][:].indirect(offsets[:, entries]), values, gates[q][:], MULT)
-
-        for e in range(E):
-            if e % 2 == 0:
-                acc = [psum.tile([P, PAIR], F32, name="acc%d" % b) for b in range(BLOCKS)]
-            expert(e, acc)
-            if e % 2 == 1 and e < E - 1:
-                for b in range(BLOCKS):
-                    scatter(e // 2, b, sums[e // 2][:, b, :])
+            nc.vector.tensor_tensor(routed[b][:].indirect(offsets[:, entries]), values, gates[:, q * PAIR:(q + 1) * PAIR], MULT)
 
         def add_and_store(b, cuts):
             for lo, hi in zip(cuts, cuts[1:]):
@@ -149,12 +152,53 @@ def tile_moe_res_lin_none_kernel(tc, x_words, x_scales, xr, w, gate, offs, out):
                 nc.sync.dma_start(out=out[b * P:(b + 1) * P, tokens], in_=resid[b][:, tokens])
 
         last = PAIRS - 1
-        scatter(last, 0, sums[last][:, 0, :])
-        add_and_store(0, (0, T // 2, T))
-        scatter(last, 1, sums[last][:, 1, :])
+        for q in range(last):
+            acc = [psum.tile([P, PAIR], F32, name="acc%d" % b) for b in range(BLOCKS)]
+            tiles = new_expert()
+            for o in range(PASSES):
+                round_blocks(tiles[0], 2 * q, o, 0, BLOCKS)
+            multiply(tiles, 2 * q, acc, 0, 2)
+            multiply(tiles, 2 * q, acc, 2, 3)
+            tiles = new_expert()
+            round_blocks(tiles[0], 2 * q + 1, 0, 0, BLOCKS)
+            for b in range(BLOCKS):
+                round_blocks(tiles[0], 2 * q + 1, 1, b, b + 1)
+                multiply(tiles, 2 * q + 1, acc, b, b + 1)
+                nc.scalar.copy(out=sums[q][:, b, :], in_=acc[b][:])
+            for b in range(BLOCKS):
+                scatter(q, b, sums[q][:, b, :])
+
+        acc = [psum.tile([P, PAIR], F32, name="acc%d" % b) for b in range(BLOCKS)]
+        both = [new_expert() for half in range(2)]
+        for b in range(BLOCKS):
+            for half in range(2):
+                for o in range(PASSES):
+                    round_blocks(both[half][0], 2 * last + half, o, b, b + 1)
+                multiply(both[half], 2 * last + half, acc, b, b + 1)
+            if b > 0:
+                nc.scalar.copy(out=sums[last][:, b - 1, :], in_=acc[b - 1][:])
+                scatter(last, b - 1, sums[last][:, b - 1, :])
+
+        turned = []
+        for c in range(CHUNKS):
+            total = psum.tile([P, per_bank, P], F32, name="bank%d" % c)
+            for source in (resid[0], routed[0]):
+                for i in range(per_bank):
+                    cols = slice(c * BANK + i * P, c * BANK + (i + 1) * P)
+                    nc.tensor.matmul(total[:, i, :], source[:, cols], identity[:], is_transpose=True,
+                                     start=(source is resid[0] and i == 0), stop=(source is routed[0] and i == per_bank - 1))
+            turned.append(keep.tile([P, per_bank, P], F32, name="turned%d" % c))
+            nc.scalar.copy(out=turned[c][:], in_=total[:])
         add_and_store(1, (0, T // 2))
-        spare = routed[0][:, T - PAIR:T]
+        spare = routed[1][:, 0:PAIR]
         nc.scalar.copy(out=spare, in_=acc[LAST_BLOCK][:])
-        scatter(last, LAST_BLOCK, spare)
         add_and_store(1, (T // 2, T))
+        scatter(last, LAST_BLOCK, spare)
+        for c in range(CHUNKS):
+            back = psum.tile([P, per_bank, P], F32, name="bank%d" % ((c - 1) % (CHUNKS + 1)))
+            for i in range(per_bank):
+                nc.tensor.transpose(back[:, i, :], turned[c][:, i, :], identity[:])
+            tokens = slice(c * BANK, (c + 1) * BANK)
+            nc.scalar.copy(out=resid[0][:, tokens], in_=back[:].rearrange("p i s -> p (i s)"))
+            nc.sync.dma_start(out=out[0:P, tokens], in_=resid[0][:, tokens])
         add_and_store(LAST_BLOCK, (0, T // 2, 3 * T // 4, T))

@@ -30,7 +30,7 @@ QUADRANT = 32
 SCALE_ROWS = 4
 RUN = 4
 CODES_DEPTH = 4
-CHUNKS = T // 512
+CHUNKS = 3
 GATE_ROW = SLOTS // P
 BANK = 512
 
@@ -83,9 +83,12 @@ def tile_moe_res_lin_none_kernel(tc, x_words, x_scales, xr, w, gate, offs, out):
         load_x(1)
         for e in range(E):
             for o in range(PASSES):
+                if (e, o) == (E - 1, 0):
+                    nc.sync.dma_start(out=resid[0][:, CHUNKS * BANK:T], in_=xr[0:P, CHUNKS * BANK:T])
                 if (e, o) not in raw:
                     load_w(e, o)
-        for b in range(BLOCKS):
+        nc.sync.dma_start(out=resid[0][:, 0:CHUNKS * BANK], in_=xr[0:P, 0:CHUNKS * BANK])
+        for b in range(1, BLOCKS):
             nc.sync.dma_start(out=resid[b][:], in_=xr[b * P:(b + 1) * P, :])
 
         nc.vector.memset(routed[0][:], 0.0)
@@ -178,6 +181,8 @@ def tile_moe_res_lin_none_kernel(tc, x_words, x_scales, xr, w, gate, offs, out):
             if b > 0:
                 nc.scalar.copy(out=sums[last][:, b - 1, :], in_=acc[b - 1][:])
                 scatter(last, b - 1, sums[last][:, b - 1, :])
+            if b == 1:
+                add_and_store(0, (CHUNKS * BANK, T))
 
         turned = []
         for c in range(CHUNKS):
@@ -200,5 +205,5 @@ def tile_moe_res_lin_none_kernel(tc, x_words, x_scales, xr, w, gate, offs, out):
                 nc.tensor.transpose(back[:, i, :], turned[c][:, i, :], identity[:])
             tokens = slice(c * BANK, (c + 1) * BANK)
             nc.scalar.copy(out=resid[0][:, tokens], in_=back[:].rearrange("p i s -> p (i s)"))
-            nc.sync.dma_start(out=out[0:P, tokens], in_=resid[0][:, tokens])
-        add_and_store(LAST_BLOCK, (0, T // 2, 3 * T // 4, T))
+            nc.scalar.dma_start(out=out[0:P, tokens], in_=resid[0][:, tokens])
+        add_and_store(LAST_BLOCK, range(0, T + 1, BANK))

@@ -29,21 +29,21 @@ LIST_ROWS = 16
 QUADRANT = 32
 SCALE_ROWS = 4
 RUN = 4
-CODES_DEPTH = 4
+CODES_DEPTH = 2
 CHUNKS = 3
 GATE_ROW = SLOTS // P
 BANK = 512
 
 
 def rounded_on_vector(e, o, b):
-    return b == LAST_BLOCK and e == 1
+    return b == LAST_BLOCK and (e == 1 or (e in (3, 5) and o == 0))
 
 
 def tile_moe_res_lin_none_kernel(tc, x_words, x_scales, xr, w, gate, offs, out):
     nc = tc.nc
     with ExitStack() as ctx:
         keep = ctx.enter_context(tc.tile_pool(name="keep", bufs=1))
-        raw_pool = ctx.enter_context(tc.tile_pool(name="raw", bufs=E * PASSES))
+        raw_pool = ctx.enter_context(tc.tile_pool(name="raw", bufs=(E - 2) * PASSES))
         ring = ctx.enter_context(tc.tile_pool(name="ring", bufs=CODES_DEPTH))
         psum = ctx.enter_context(tc.psum_pool(name="psum", bufs=1))
 
@@ -61,10 +61,14 @@ def tile_moe_res_lin_none_kernel(tc, x_words, x_scales, xr, w, gate, offs, out):
         sums = [keep.tile([P, BLOCKS, PAIR], F32, name="sums%d" % q) for q in range(PAIRS)]
 
         raw = {}
+        raw_last = keep.tile([P, 2 * PASSES, PACK, N], F32, name="raw_last")
 
         def load_w(e, o):
-            raw[e, o] = raw_pool.tile([P, PACK, N], F32, name="raw")
-            nc.sync.dma_start(out=raw[e, o][:], in_=w[e, o * K_PASS:(o + 1) * K_PASS, :].rearrange("(p t) n -> p t n", t=PACK))
+            if e < E - 2:
+                raw[e, o] = raw_pool.tile([P, PACK, N], F32, name="raw")[:]
+            else:
+                raw[e, o] = raw_last[:, (e % 2) * PASSES + o, :, :]
+            nc.sync.dma_start(out=raw[e, o], in_=w[e, o * K_PASS:(o + 1) * K_PASS, :].rearrange("(p t) n -> p t n", t=PACK))
 
         def load_x(o):
             nc.sync.dma_start(out=token_words[o][:], in_=x_words[o].rearrange("p t r -> p (t r)").bitcast(I32))
@@ -111,7 +115,7 @@ def tile_moe_res_lin_none_kernel(tc, x_words, x_scales, xr, w, gate, offs, out):
 
         def interleave(engine_copy, grouped, e, o, b0, b1):
             engine_copy(
-                out=grouped[:, b0:b1, o, :].rearrange("p b (c i t) -> p b c t i", i=RUN, t=PACK),
+                out=grouped[:, b0:b1, (e % 2) * PASSES + o, :].rearrange("p b (c i t) -> p b c t i", i=RUN, t=PACK),
                 in_=raw[e, o][:, :, b0 * P:b1 * P].rearrange("p t (b c i) -> p b c t i", i=RUN, b=b1 - b0),
             )
 
@@ -122,24 +126,24 @@ def tile_moe_res_lin_none_kernel(tc, x_words, x_scales, xr, w, gate, offs, out):
             if b1 > b0:
                 interleave(nc.scalar.copy, grouped, e, o, b0, b1)
 
-        def new_expert():
-            grouped = ring.tile([P, BLOCKS, PASSES, P * PACK], BF16, name="grouped", align_bytes=64)
-            codes = ring.tile([P, BLOCKS * PASSES * P], U32, name="codes", align_bytes=64)
-            scales = ring.tile([P, BLOCKS * PASSES * P], U8, name="scales", align_bytes=64)
+        def new_pair():
+            grouped = ring.tile([P, BLOCKS, 2 * PASSES, K_PASS], BF16, name="grouped", align_bytes=64)
+            codes = ring.tile([P, BLOCKS, 2 * PASSES * P], U32, name="codes", align_bytes=64)
+            scales = ring.tile([P, BLOCKS, 2 * PASSES * P], U8, name="scales", align_bytes=64)
             return grouped, codes, scales
 
-        def multiply(tiles, e, acc, b0, b1):
+        def multiply(tiles, e0, e1, acc, b):
             grouped, codes, scales = tiles
-            slots = slice(e * C, (e + 1) * C)
-            place = slice((e % 2) * C, (e % 2 + 1) * C)
-            run_cols = slice(b0 * PASSES * P, b1 * PASSES * P)
-            nc.vector.quantize_mx(out=codes[:, run_cols].bitcast(FP8X4), scales=scales[:, run_cols],
-                                  in_=grouped[:, b0:b1, :, :].rearrange("p b o x -> p (b o x)"))
-            for b in range(b0, b1):
+            u0, u1 = (e0 % 2) * PASSES, ((e1 - 1) % 2 + 1) * PASSES
+            nc.vector.quantize_mx(out=codes[:, b, u0 * P:u1 * P].bitcast(FP8X4), scales=scales[:, b, u0 * P:u1 * P],
+                                  in_=grouped[:, b, u0:u1, :].rearrange("p u x -> p (u x)"))
+            for e in range(e0, e1):
+                slots = slice(e * C, (e + 1) * C)
                 for o in range(PASSES):
-                    w_cols = slice((b * PASSES + o) * P, (b * PASSES + o + 1) * P)
-                    nc.tensor.matmul_mx(out=acc[b][:, place],
-                                        lhsT=codes[:, w_cols].bitcast(FP8X4), lhsT_scale=scales[:, w_cols],
+                    unit = (e % 2) * PASSES + o
+                    w_cols = slice(unit * P, (unit + 1) * P)
+                    nc.tensor.matmul_mx(out=acc[b][:, (e % 2) * C:(e % 2 + 1) * C],
+                                        lhsT=codes[:, b, w_cols].bitcast(FP8X4), lhsT_scale=scales[:, b, w_cols],
                                         rhs=slot_words[o][:, slots].bitcast(FP8X4),
                                         rhs_scale=slot_scales[SCALE_ROWS * o:P, slots],
                                         start=(o == 0), stop=(o == PASSES - 1))
@@ -157,53 +161,69 @@ def tile_moe_res_lin_none_kernel(tc, x_words, x_scales, xr, w, gate, offs, out):
         last = PAIRS - 1
         for q in range(last):
             acc = [psum.tile([P, PAIR], F32, name="acc%d" % b) for b in range(BLOCKS)]
-            tiles = new_expert()
+            tiles = new_pair()
+            first, second = 2 * q, 2 * q + 1
+            alone = BLOCKS if q == 0 else 1
             for o in range(PASSES):
-                round_blocks(tiles[0], 2 * q, o, 0, BLOCKS)
-            multiply(tiles, 2 * q, acc, 0, 2)
-            multiply(tiles, 2 * q, acc, 2, 3)
-            tiles = new_expert()
-            round_blocks(tiles[0], 2 * q + 1, 0, 0, BLOCKS)
+                round_blocks(tiles[0], first, o, 0, BLOCKS)
+            for b in range(alone):
+                multiply(tiles, first, second, acc, b)
+            round_blocks(tiles[0], second, 0, 0, BLOCKS)
             for b in range(BLOCKS):
-                round_blocks(tiles[0], 2 * q + 1, 1, b, b + 1)
-                multiply(tiles, 2 * q + 1, acc, b, b + 1)
+                round_blocks(tiles[0], second, 1, b, b + 1)
+                multiply(tiles, second if b < alone else first, second + 1, acc, b)
                 nc.scalar.copy(out=sums[q][:, b, :], in_=acc[b][:])
             for b in range(BLOCKS):
                 scatter(q, b, sums[q][:, b, :])
 
         acc = [psum.tile([P, PAIR], F32, name="acc%d" % b) for b in range(BLOCKS)]
-        both = [new_expert() for half in range(2)]
-        for b in range(BLOCKS):
-            for half in range(2):
-                for o in range(PASSES):
-                    round_blocks(both[half][0], 2 * last + half, o, b, b + 1)
-                multiply(both[half], 2 * last + half, acc, b, b + 1)
-            if b > 0:
-                nc.scalar.copy(out=sums[last][:, b - 1, :], in_=acc[b - 1][:])
-                scatter(last, b - 1, sums[last][:, b - 1, :])
+        tiles = new_pair()
+        for e in (E - 2, E - 1):
+            for o in range(PASSES):
+                round_blocks(tiles[0], e, o, 0, 1)
+            multiply(tiles, e, e + 1, acc, 0)
+        for b in range(1, BLOCKS):
+            nc.scalar.copy(
+                out=tiles[0][:, b, :, :].rearrange("p u (c i t) -> p u c t i", i=RUN, t=PACK),
+                in_=raw_last[:, :, :, b * P:(b + 1) * P].rearrange("p u t (c i) -> p u c t i", i=RUN),
+            )
+            multiply(tiles, E - 2, E, acc, b)
+            nc.scalar.copy(out=sums[last][:, b - 1, :], in_=acc[b - 1][:])
+            scatter(last, b - 1, sums[last][:, b - 1, :])
             if b == 1:
                 add_and_store(0, (CHUNKS * BANK, T))
 
-        turned = []
-        for c in range(CHUNKS):
-            total = psum.tile([P, per_bank, P], F32, name="bank%d" % c)
-            for source in (resid[0], routed[0]):
+        turns = [(0, c) for c in range(CHUNKS)] + [(1, c) for c in range(4 - 1, 4)]
+        turned = [keep.tile([P, per_bank, P], F32, name="turned%d" % j) for j in range(len(turns))]
+
+        def turn(j):
+            b, c = turns[j]
+            total = psum.tile([P, per_bank, P], F32, name="bank%d" % j)
+            for source in (resid[b], routed[b]):
                 for i in range(per_bank):
                     cols = slice(c * BANK + i * P, c * BANK + (i + 1) * P)
                     nc.tensor.matmul(total[:, i, :], source[:, cols], identity[:], is_transpose=True,
-                                     start=(source is resid[0] and i == 0), stop=(source is routed[0] and i == per_bank - 1))
-            turned.append(keep.tile([P, per_bank, P], F32, name="turned%d" % c))
-            nc.scalar.copy(out=turned[c][:], in_=total[:])
-        add_and_store(1, (0, T // 2))
+                                     start=(source is resid[b] and i == 0), stop=(source is routed[b] and i == per_bank - 1))
+            nc.scalar.copy(out=turned[j][:], in_=total[:])
+
+        def turn_back(j):
+            b, c = turns[j]
+            back = psum.tile([P, per_bank, P], F32, name="bank%d" % (j - 1) if j > 0 else "acc0")
+            for i in range(per_bank):
+                nc.tensor.transpose(back[:, i, :], turned[j][:, i, :], identity[:])
+            tokens = slice(c * BANK, (c + 1) * BANK)
+            nc.scalar.copy(out=resid[b][:, tokens], in_=back[:].rearrange("p i s -> p (i s)"))
+            nc.scalar.dma_start(out=out[b * P:(b + 1) * P, tokens], in_=resid[b][:, tokens])
+
+        for j in range(CHUNKS):
+            turn(j)
+        add_and_store(1, (0, BANK))
         spare = routed[1][:, 0:PAIR]
         nc.scalar.copy(out=spare, in_=acc[LAST_BLOCK][:])
-        add_and_store(1, (T // 2, T))
+        add_and_store(1, (BANK, CHUNKS * BANK))
         scatter(last, LAST_BLOCK, spare)
-        for c in range(CHUNKS):
-            back = psum.tile([P, per_bank, P], F32, name="bank%d" % ((c - 1) % (CHUNKS + 1)))
-            for i in range(per_bank):
-                nc.tensor.transpose(back[:, i, :], turned[c][:, i, :], identity[:])
-            tokens = slice(c * BANK, (c + 1) * BANK)
-            nc.scalar.copy(out=resid[0][:, tokens], in_=back[:].rearrange("p i s -> p (i s)"))
-            nc.scalar.dma_start(out=out[0:P, tokens], in_=resid[0][:, tokens])
+        turn_back(0)
+        turn(CHUNKS)
+        for j in range(1, len(turns)):
+            turn_back(j)
         add_and_store(LAST_BLOCK, range(0, T + 1, BANK))

@@ -15,6 +15,7 @@ U8 = mybir.dt.uint8
 FP8X4 = mybir.dt.float8_e4m3fn_x4
 MULT = mybir.AluOpType.mult
 ADD = mybir.AluOpType.add
+COPY = mybir.ActivationFunctionType.Copy
 
 P = 128
 PACK = 4
@@ -30,20 +31,16 @@ QUADRANT = 32
 SCALE_ROWS = 4
 RUN = 4
 CODES_DEPTH = 2
-CHUNKS = 3
-GATE_ROW = SLOTS // P
+CALLS = (((0, 0), (0, 1)), ((1, 0),), ((1, 1),), ((0, 2), (1, 2)))
+PRODUCTS = (((0, 0),), ((1, 0),), ((1, 1), (0, 1)), ((0, 2), (1, 2)))
+PLACE = {part: (i, j) for i, call in enumerate(CALLS) for j, part in enumerate(call)}
 BANK = 512
-
-
-def rounded_on_vector(e, o, b):
-    return b == LAST_BLOCK and (e == 1 or (e in (3, 5) and o == 0))
 
 
 def tile_moe_res_lin_none_kernel(tc, x_words, x_scales, xr, w, gate, offs, out):
     nc = tc.nc
     with ExitStack() as ctx:
         keep = ctx.enter_context(tc.tile_pool(name="keep", bufs=1))
-        raw_pool = ctx.enter_context(tc.tile_pool(name="raw", bufs=(E - 2) * PASSES))
         ring = ctx.enter_context(tc.tile_pool(name="ring", bufs=CODES_DEPTH))
         psum = ctx.enter_context(tc.psum_pool(name="psum", bufs=1))
 
@@ -53,29 +50,29 @@ def tile_moe_res_lin_none_kernel(tc, x_words, x_scales, xr, w, gate, offs, out):
         token_words = [keep.tile([P, T], I32, name="token_words%d" % o) for o in range(PASSES)]
         slot_words = [keep.tile([P, SLOTS], U32, name="slot_words%d" % o, align_bytes=64) for o in range(PASSES)]
         slot_scales = keep.tile([P, SLOTS], U8, name="slot_scales", align_bytes=64)
-        gate_row = keep.tile([P, GATE_ROW], F32, name="gate_row")
+        gate_rows = keep.tile([P, C], F32, name="gate_rows")
+        gate_cols = keep.tile([P, E], F32, name="gate_cols")
         gates = keep.tile([P, SLOTS], F32, name="gates")
         identity = keep.tile([P, P], F32, name="identity")
         routed = [keep.tile([P, T], F32, name="routed%d" % b) for b in range(BLOCKS)]
         resid = [keep.tile([P, T], F32, name="resid%d" % b) for b in range(BLOCKS)]
-        sums = [keep.tile([P, BLOCKS, PAIR], F32, name="sums%d" % q) for q in range(PAIRS)]
+        raw = [keep.tile([P, PASSES, PACK, N], F32, name="raw%d" % e) for e in range(E)]
+        rounded = [[keep.tile([P, len(call) * PASSES * K_PASS], BF16, name="rounded%d_%d" % (s, i), align_bytes=64)
+                    for i, call in enumerate(CALLS)] for s in range(CODES_DEPTH)]
 
-        raw = {}
-        raw_last = keep.tile([P, 2 * PASSES, PACK, N], F32, name="raw_last")
+        def pieces(e, b):
+            i, j = PLACE[e % 2, b]
+            return rounded[e // 2 % CODES_DEPTH][i][:, j * PASSES * K_PASS:(j + 1) * PASSES * K_PASS]
 
         def load_w(e, o):
-            if e < E - 2:
-                raw[e, o] = raw_pool.tile([P, PACK, N], F32, name="raw")[:]
-            else:
-                raw[e, o] = raw_last[:, (e % 2) * PASSES + o, :, :]
-            nc.sync.dma_start(out=raw[e, o], in_=w[e, o * K_PASS:(o + 1) * K_PASS, :].rearrange("(p t) n -> p t n", t=PACK))
+            nc.sync.dma_start(out=raw[e][:, o], in_=w[e, o * K_PASS:(o + 1) * K_PASS, :].rearrange("(p t) n -> p t n", t=PACK))
 
         def load_x(o):
             nc.sync.dma_start(out=token_words[o][:], in_=x_words[o].rearrange("p t r -> p (t r)").bitcast(I32))
 
         nc.vector.memset(token_scales[:].bitcast(I32), 0)
         nc.sync.dma_start(offsets[:], offs)
-        nc.sync.dma_start(out=gate_row[:], in_=gate[0, :].rearrange("(p i) -> p i", i=GATE_ROW))
+        nc.sync.dma_start(out=gate_rows[:], in_=gate[0:P // E, :].rearrange("r (e c) -> (r e) c", c=C))
         for quad in range(P // QUADRANT):
             rows = slice(QUADRANT * quad, QUADRANT * quad + SCALE_ROWS * PASSES)
             nc.sync.dma_start(out=landed_scales[rows, :].bitcast(I32),
@@ -87,12 +84,9 @@ def tile_moe_res_lin_none_kernel(tc, x_words, x_scales, xr, w, gate, offs, out):
         load_x(1)
         for e in range(E):
             for o in range(PASSES):
-                if (e, o) == (E - 1, 0):
-                    nc.sync.dma_start(out=resid[0][:, CHUNKS * BANK:T], in_=xr[0:P, CHUNKS * BANK:T])
-                if (e, o) not in raw:
+                if (e, o) != (0, 0):
                     load_w(e, o)
-        nc.sync.dma_start(out=resid[0][:, 0:CHUNKS * BANK], in_=xr[0:P, 0:CHUNKS * BANK])
-        for b in range(1, BLOCKS):
+        for b in range(BLOCKS):
             nc.sync.dma_start(out=resid[b][:], in_=xr[b * P:(b + 1) * P, :])
 
         nc.vector.memset(routed[0][:], 0.0)
@@ -101,99 +95,101 @@ def tile_moe_res_lin_none_kernel(tc, x_words, x_scales, xr, w, gate, offs, out):
 
         make_identity(nc, identity[:])
         per_bank = BANK // P
-        for h in range(GATE_ROW // per_bank):
+        columns = psum.tile([P, P], F32, name="back1")
+        nc.tensor.transpose(columns[:], gate_rows[:], identity[:])
+        nc.scalar.activation(out=gate_cols[:], in_=columns[:, 0:E], func=COPY)
+        for h in range(E // per_bank):
             spread = psum.tile([P, per_bank, P], F32, name="bank%d" % h)
             for i in range(per_bank):
-                column = h * per_bank + i
-                nc.tensor.transpose(spread[:, i, :], gate_row[:, column:column + 1].to_broadcast([P, P]), identity[:])
-            nc.scalar.copy(out=gates[:].rearrange("p (s i) -> p s i", i=GATE_ROW)[:, :, h * per_bank:(h + 1) * per_bank],
-                           in_=spread[:].rearrange("p i s -> p s i"))
+                e = h * per_bank + i
+                nc.tensor.transpose(spread[:, i, :], gate_cols[:, e:e + 1].to_broadcast([P, P]), identity[:])
+            nc.scalar.copy(out=gates[:, h * BANK:(h + 1) * BANK], in_=spread[:].rearrange("p i s -> p (i s)"))
 
         nc.vector.tensor_copy(slot_scales[:], token_scales[:].indirect(offsets[:]))
         for o in range(PASSES):
             nc.vector.tensor_copy(slot_words[o][:], token_words[o][:].bitcast(U32).indirect(offsets[:]))
 
-        def interleave(engine_copy, grouped, e, o, b0, b1):
+        def interleave(engine_copy, e, o, b):
             engine_copy(
-                out=grouped[:, b0:b1, (e % 2) * PASSES + o, :].rearrange("p b (c i t) -> p b c t i", i=RUN, t=PACK),
-                in_=raw[e, o][:, :, b0 * P:b1 * P].rearrange("p t (b c i) -> p b c t i", i=RUN, b=b1 - b0),
+                out=pieces(e, b)[:, o * K_PASS:(o + 1) * K_PASS].rearrange("p (c i t) -> p c t i", i=RUN, t=PACK),
+                in_=raw[e][:, o, :, b * P:(b + 1) * P].rearrange("p t (c i) -> p c t i", i=RUN),
             )
 
-        def round_blocks(grouped, e, o, b0, b1):
-            if rounded_on_vector(e, o, b1 - 1):
-                interleave(nc.vector.tensor_copy, grouped, e, o, b1 - 1, b1)
-                b1 = b1 - 1
-            if b1 > b0:
-                interleave(nc.scalar.copy, grouped, e, o, b0, b1)
+        def interleave_on_gpsimd(e, b):
+            nc.gpsimd.tensor_scalar(
+                out=pieces(e, b).rearrange("p (o n t) -> p o n t", o=PASSES, t=PACK),
+                in0=raw[e][:, :, :, b * P:(b + 1) * P].rearrange("p o t n -> p o n t"),
+                scalar1=1.0, scalar2=0.0, op0=MULT, op1=ADD)
 
-        def new_pair():
-            grouped = ring.tile([P, BLOCKS, 2 * PASSES, K_PASS], BF16, name="grouped", align_bytes=64)
-            codes = ring.tile([P, BLOCKS, 2 * PASSES * P], U32, name="codes", align_bytes=64)
-            scales = ring.tile([P, BLOCKS, 2 * PASSES * P], U8, name="scales", align_bytes=64)
-            return grouped, codes, scales
+        made = {}
 
-        def multiply(tiles, e0, e1, acc, b):
-            grouped, codes, scales = tiles
-            u0, u1 = (e0 % 2) * PASSES, ((e1 - 1) % 2 + 1) * PASSES
-            nc.vector.quantize_mx(out=codes[:, b, u0 * P:u1 * P].bitcast(FP8X4), scales=scales[:, b, u0 * P:u1 * P],
-                                  in_=grouped[:, b, u0:u1, :].rearrange("p u x -> p (u x)"))
-            for e in range(e0, e1):
-                slots = slice(e * C, (e + 1) * C)
-                for o in range(PASSES):
-                    unit = (e % 2) * PASSES + o
-                    w_cols = slice(unit * P, (unit + 1) * P)
-                    nc.tensor.matmul_mx(out=acc[b][:, (e % 2) * C:(e % 2 + 1) * C],
-                                        lhsT=codes[:, b, w_cols].bitcast(FP8X4), lhsT_scale=scales[:, b, w_cols],
-                                        rhs=slot_words[o][:, slots].bitcast(FP8X4),
-                                        rhs_scale=slot_scales[SCALE_ROWS * o:P, slots],
-                                        start=(o == 0), stop=(o == PASSES - 1))
+        def quantise_and_multiply(q, i, acc):
+            width = len(CALLS[i]) * PASSES * P
+            codes = ring.tile([P, width], U32, name="codes%d" % i, align_bytes=64)
+            scales = ring.tile([P, width], U8, name="scales%d" % i, align_bytes=64)
+            nc.vector.quantize_mx(out=codes[:].bitcast(FP8X4), scales=scales[:], in_=rounded[q % CODES_DEPTH][i][:])
+            for j, (h, b) in enumerate(CALLS[i]):
+                made[h, b] = (codes, scales, j)
+            for h, b in PRODUCTS[i]:
+                multiply(*made[h, b], 2 * q + h, acc[b], b > 0)
 
-        def scatter(q, b, values):
+        def multiply(codes, scales, j, e, acc, tokens_stationary):
+            slots = slice(e * C, (e + 1) * C)
+            for o in range(PASSES):
+                w_cols = slice((j * PASSES + o) * P, (j * PASSES + o + 1) * P)
+                weights = (codes[:, w_cols].bitcast(FP8X4), scales[:, w_cols])
+                tokens = (slot_words[o][:, slots].bitcast(FP8X4), slot_scales[SCALE_ROWS * o:P, slots])
+                fixed, moving = (tokens, weights) if tokens_stationary else (weights, tokens)
+                nc.tensor.matmul_mx(out=acc[:, (e % 2) * C:(e % 2 + 1) * C], lhsT=fixed[0], lhsT_scale=fixed[1],
+                                    rhs=moving[0], rhs_scale=moving[1], start=(o == 0), stop=(o == PASSES - 1))
+
+        def window(q, b):
             entries = slice(q * PAIR // LIST_ROWS, (q + 1) * PAIR // LIST_ROWS)
-            nc.vector.tensor_tensor(routed[b][:].indirect(offsets[:, entries]), values, gates[:, q * PAIR:(q + 1) * PAIR], MULT)
+            return routed[b][:].indirect(offsets[:, entries])
 
-        def add_and_store(b, cuts):
-            for lo, hi in zip(cuts, cuts[1:]):
-                tokens = slice(lo, hi)
-                nc.vector.tensor_tensor(resid[b][:, tokens], resid[b][:, tokens], routed[b][:, tokens], ADD)
-                nc.sync.dma_start(out=out[b * P:(b + 1) * P, tokens], in_=resid[b][:, tokens])
+        def gate_and_turn(e, acc, gated, back):
+            cols = slice((e % 2) * C, (e % 2 + 1) * C)
+            nc.scalar.activation(out=gated[:, cols], in_=acc[:, cols], func=COPY, scale=gate_cols[:, e:e + 1])
+            nc.tensor.transpose(back[:, cols], gated[:, cols], identity[:])
 
         last = PAIRS - 1
-        for q in range(last):
-            acc = [psum.tile([P, PAIR], F32, name="acc%d" % b) for b in range(BLOCKS)]
-            tiles = new_pair()
+        for q in range(PAIRS):
             first, second = 2 * q, 2 * q + 1
-            alone = BLOCKS if q == 0 else 1
+            acc = [psum.tile([P, PAIR], F32, name="acc%d" % b) for b in range(BLOCKS)]
+            back = {b: psum.tile([P, PAIR], F32, name="back%d" % b) for b in range(1, BLOCKS)}
+            gated = {b: ring.tile([P, PAIR], F32, name="gated%d" % b) for b in range(1, BLOCKS)}
             for o in range(PASSES):
-                round_blocks(tiles[0], first, o, 0, BLOCKS)
-            for b in range(alone):
-                multiply(tiles, first, second, acc, b)
-            round_blocks(tiles[0], second, 0, 0, BLOCKS)
-            for b in range(BLOCKS):
-                round_blocks(tiles[0], second, 1, b, b + 1)
-                multiply(tiles, second if b < alone else first, second + 1, acc, b)
-                nc.scalar.copy(out=sums[q][:, b, :], in_=acc[b][:])
-            for b in range(BLOCKS):
-                scatter(q, b, sums[q][:, b, :])
-
-        acc = [psum.tile([P, PAIR], F32, name="acc%d" % b) for b in range(BLOCKS)]
-        tiles = new_pair()
-        for e in (E - 2, E - 1):
+                for b in range(BLOCKS if q == 0 else 1):
+                    interleave(nc.scalar.copy, first, o, b)
+            if q > 0:
+                interleave_on_gpsimd(first, 2)
+                interleave_on_gpsimd(first, 1)
+            quantise_and_multiply(q, 0, acc)
             for o in range(PASSES):
-                round_blocks(tiles[0], e, o, 0, 1)
-            multiply(tiles, e, e + 1, acc, 0)
-        for b in range(1, BLOCKS):
-            nc.scalar.copy(
-                out=tiles[0][:, b, :, :].rearrange("p u (c i t) -> p u c t i", i=RUN, t=PACK),
-                in_=raw_last[:, :, :, b * P:(b + 1) * P].rearrange("p u t (c i) -> p u c t i", i=RUN),
-            )
-            multiply(tiles, E - 2, E, acc, b)
-            nc.scalar.copy(out=sums[last][:, b - 1, :], in_=acc[b - 1][:])
-            scatter(last, b - 1, sums[last][:, b - 1, :])
-            if b == 1:
-                add_and_store(0, (CHUNKS * BANK, T))
+                for b in range(BLOCKS):
+                    interleave(nc.vector.tensor_copy if (q, b) == (0, LAST_BLOCK) else nc.scalar.copy, second, o, b)
+                    if o == PASSES - 1:
+                        quantise_and_multiply(q, b + 1, acc)
+            for b in range(BLOCKS):
+                if b == 0 and q < last:
+                    values = pieces(first + 2, LAST_BLOCK)[:, 0:2 * PAIR].bitcast(F32)
+                else:
+                    values = ring.tile([P, PAIR], F32, name="sums%d" % b)[:]
+                if b == 0:
+                    nc.scalar.copy(out=values, in_=acc[b][:])
+                    nc.vector.tensor_tensor(window(q, b), values, gates[:, q * PAIR:(q + 1) * PAIR], MULT)
+                else:
+                    for e in (first, second):
+                        gate_and_turn(e, acc[b], gated[b], back[b])
+                    nc.scalar.copy(out=values, in_=back[b][:])
+                    nc.vector.tensor_copy(window(q, b), values)
 
-        turns = [(0, c) for c in range(CHUNKS)] + [(1, c) for c in range(4 - 1, 4)]
+        def add_and_store(engine, queue, b, lo, hi):
+            tokens = slice(lo, hi)
+            engine.tensor_tensor(resid[b][:, tokens], resid[b][:, tokens], routed[b][:, tokens], ADD)
+            queue.dma_start(out=out[b * P:(b + 1) * P, tokens], in_=resid[b][:, tokens])
+
+        turns = [(0, 2), (0, 3), (1, 3)]
         turned = [keep.tile([P, per_bank, P], F32, name="turned%d" % j) for j in range(len(turns))]
 
         def turn(j):
@@ -208,22 +204,22 @@ def tile_moe_res_lin_none_kernel(tc, x_words, x_scales, xr, w, gate, offs, out):
 
         def turn_back(j):
             b, c = turns[j]
-            back = psum.tile([P, per_bank, P], F32, name="bank%d" % (j - 1) if j > 0 else "acc0")
+            back = psum.tile([P, per_bank, P], F32, name="bank%d" % (j - 1) if j > 0 else "acc1")
             for i in range(per_bank):
                 nc.tensor.transpose(back[:, i, :], turned[j][:, i, :], identity[:])
             tokens = slice(c * BANK, (c + 1) * BANK)
             nc.scalar.copy(out=resid[b][:, tokens], in_=back[:].rearrange("p i s -> p (i s)"))
             nc.scalar.dma_start(out=out[b * P:(b + 1) * P, tokens], in_=resid[b][:, tokens])
 
-        for j in range(CHUNKS):
-            turn(j)
-        add_and_store(1, (0, BANK))
-        spare = routed[1][:, 0:PAIR]
-        nc.scalar.copy(out=spare, in_=acc[LAST_BLOCK][:])
-        add_and_store(1, (BANK, CHUNKS * BANK))
-        scatter(last, LAST_BLOCK, spare)
+        turn(0)
+        turn(1)
+        add_and_store(nc.gpsimd, nc.scalar, 0, 0, BANK)
         turn_back(0)
-        turn(CHUNKS)
-        for j in range(1, len(turns)):
-            turn_back(j)
-        add_and_store(LAST_BLOCK, range(0, T + 1, BANK))
+        add_and_store(nc.gpsimd, nc.scalar, 0, BANK, 2 * BANK)
+        turn_back(1)
+        turn(2)
+        turn_back(2)
+        for lo, hi in ((0, 768), (768, 1536)):
+            add_and_store(nc.vector, nc.sync, 1, lo, hi)
+        for lo, hi in ((0, 768), (768, 1536), (1536, T)):
+            add_and_store(nc.vector, nc.sync, LAST_BLOCK, lo, hi)

@@ -89,9 +89,11 @@ def tile_moe_res_lin_none_kernel(tc, x_words, x_scales, xr, w, gate, offs, out):
         for b in range(BLOCKS):
             nc.sync.dma_start(out=resid[b][:], in_=xr[b * P:(b + 1) * P, :])
 
-        nc.vector.memset(routed[0][:], 0.0)
-        for b in range(1, BLOCKS):
-            nc.scalar.copy(out=routed[b][:], in_=routed[0][:])
+        zeros = keep.tile([P, P], F32, name="zeros")
+        nc.vector.memset(zeros[:], 0.0)
+        for b in range(BLOCKS):
+            copy = nc.scalar.copy if b == LAST_BLOCK else nc.vector.tensor_copy
+            copy(out=routed[b][:].rearrange("p (r c) -> p r c", c=P), in_=zeros[:].unsqueeze(1).to_broadcast([P, T // P, P]))
 
         make_identity(nc, identity[:])
         per_bank = BANK // P
@@ -158,16 +160,19 @@ def tile_moe_res_lin_none_kernel(tc, x_words, x_scales, xr, w, gate, offs, out):
             acc = [psum.tile([P, PAIR], F32, name="acc%d" % b) for b in range(BLOCKS)]
             back = {b: psum.tile([P, PAIR], F32, name="back%d" % b) for b in range(1, BLOCKS)}
             gated = {b: ring.tile([P, PAIR], F32, name="gated%d" % b) for b in range(1, BLOCKS)}
-            for o in range(PASSES):
-                for b in range(BLOCKS if q == 0 else 1):
-                    interleave(nc.scalar.copy, first, o, b)
-            if q > 0:
+            if q == 0:
+                for o in range(PASSES):
+                    for b in range(BLOCKS):
+                        interleave(nc.scalar.copy, first, o, b)
+            else:
+                nc.scalar.copy(out=pieces(first, 0).rearrange("p (o c i t) -> p o c t i", o=PASSES, i=RUN, t=PACK),
+                               in_=raw[first][:, :, :, 0:P].rearrange("p o t (c i) -> p o c t i", i=RUN))
                 interleave_on_gpsimd(first, 2)
                 interleave_on_gpsimd(first, 1)
             quantise_and_multiply(q, 0, acc)
             for o in range(PASSES):
                 for b in range(BLOCKS):
-                    interleave(nc.vector.tensor_copy if (q, b) == (0, LAST_BLOCK) else nc.scalar.copy, second, o, b)
+                    interleave(nc.vector.tensor_copy if q == 0 and (o, b) in ((0, LAST_BLOCK), (1, 0)) else nc.scalar.copy, second, o, b)
                     if o == PASSES - 1:
                         quantise_and_multiply(q, b + 1, acc)
             for b in range(BLOCKS):
@@ -184,42 +189,44 @@ def tile_moe_res_lin_none_kernel(tc, x_words, x_scales, xr, w, gate, offs, out):
                     nc.scalar.copy(out=values, in_=back[b][:])
                     nc.vector.tensor_copy(window(q, b), values)
 
-        def add_and_store(engine, queue, b, lo, hi):
+        def add_and_store(engine, b, lo, hi, total):
             tokens = slice(lo, hi)
-            engine.tensor_tensor(resid[b][:, tokens], resid[b][:, tokens], routed[b][:, tokens], ADD)
-            queue.dma_start(out=out[b * P:(b + 1) * P, tokens], in_=resid[b][:, tokens])
+            engine.tensor_tensor(total, resid[b][:, tokens], routed[b][:, tokens], ADD)
+            nc.sync.dma_start(out=out[b * P:(b + 1) * P, tokens], in_=total)
 
-        turns = [(0, 2), (0, 3), (1, 3)]
-        turned = [keep.tile([P, per_bank, P], F32, name="turned%d" % j) for j in range(len(turns))]
+        turns = [(0, 2), (0, 3), (1, 2), (1, 3)]
+        turned = [keep.tile([P, 2, per_bank, P], F32, name="turned%d" % j) for j in range(len(turns) // 2)]
 
         def turn(j):
             b, c = turns[j]
-            total = psum.tile([P, per_bank, P], F32, name="bank%d" % j)
+            total = psum.tile([P, per_bank, P], F32, name="bank%d" % j if j < len(turns) - 1 else "acc0")
             for source in (resid[b], routed[b]):
                 for i in range(per_bank):
                     cols = slice(c * BANK + i * P, c * BANK + (i + 1) * P)
                     nc.tensor.matmul(total[:, i, :], source[:, cols], identity[:], is_transpose=True,
                                      start=(source is resid[b] and i == 0), stop=(source is routed[b] and i == per_bank - 1))
-            nc.scalar.copy(out=turned[j][:], in_=total[:])
+            nc.scalar.copy(out=turned[j // 2][:, j % 2], in_=total[:])
 
         def turn_back(j):
             b, c = turns[j]
             back = psum.tile([P, per_bank, P], F32, name="bank%d" % (j - 1) if j > 0 else "acc1")
             for i in range(per_bank):
-                nc.tensor.transpose(back[:, i, :], turned[j][:, i, :], identity[:])
+                nc.tensor.transpose(back[:, i, :], turned[j // 2][:, j % 2, i, :], identity[:])
             tokens = slice(c * BANK, (c + 1) * BANK)
             nc.scalar.copy(out=resid[b][:, tokens], in_=back[:].rearrange("p i s -> p (i s)"))
-            nc.scalar.dma_start(out=out[b * P:(b + 1) * P, tokens], in_=resid[b][:, tokens])
+            nc.sync.dma_start(out=out[b * P:(b + 1) * P, tokens], in_=resid[b][:, tokens])
 
+        for c in range(2):
+            add_and_store(nc.gpsimd, 0, c * BANK, (c + 1) * BANK, resid[0][:, c * BANK:(c + 1) * BANK])
         turn(0)
         turn(1)
-        add_and_store(nc.gpsimd, nc.scalar, 0, 0, BANK)
         turn_back(0)
-        add_and_store(nc.gpsimd, nc.scalar, 0, BANK, 2 * BANK)
-        turn_back(1)
         turn(2)
+        turn_back(1)
+        turn(3)
         turn_back(2)
-        for lo, hi in ((0, 768), (768, 1536)):
-            add_and_store(nc.vector, nc.sync, 1, lo, hi)
-        for lo, hi in ((0, 768), (768, 1536), (1536, T)):
-            add_and_store(nc.vector, nc.sync, LAST_BLOCK, lo, hi)
+        turn_back(3)
+        for c in range(2):
+            add_and_store(nc.vector, 1, c * BANK, (c + 1) * BANK, turned[0][:, c].rearrange("p i s -> p (i s)"))
+        for c in range(T // BANK):
+            add_and_store(nc.vector, LAST_BLOCK, c * BANK, (c + 1) * BANK, resid[LAST_BLOCK][:, c * BANK:(c + 1) * BANK])

@@ -31,9 +31,12 @@ QUADRANT = 32
 SCALE_ROWS = 4
 RUN = 4
 CODES_DEPTH = 2
-CALLS = (((0, 0), (0, 1)), ((1, 0),), ((1, 1),), ((0, 2), (1, 2)))
-PRODUCTS = (((0, 0),), ((1, 0),), ((1, 1), (0, 1)), ((0, 2), (1, 2)))
-PLACE = {part: (i, j) for i, call in enumerate(CALLS) for j, part in enumerate(call)}
+LAYOUTS = (((0, 0, 0), (0, 0, 1), (0, 1, 0), (0, 1, 1)),
+           ((1, 0, 1), (1, 0, 0), (1, 1, 0), (1, 1, 1)),
+           ((0, 2, 0), (0, 2, 1), (1, 2, 0), (1, 2, 1)))
+CALLS = ((0, 0, 4), (1, 0, 2), (1, 2, 4), (2, 0, 4))
+PLACE = {piece: (i, j) for i, layout in enumerate(LAYOUTS) for j, piece in enumerate(layout)}
+GATE_ROW = SLOTS // P
 BANK = 512
 
 
@@ -50,19 +53,19 @@ def tile_moe_res_lin_none_kernel(tc, x_words, x_scales, xr, w, gate, offs, out):
         token_words = [keep.tile([P, T], I32, name="token_words%d" % o) for o in range(PASSES)]
         slot_words = [keep.tile([P, SLOTS], U32, name="slot_words%d" % o, align_bytes=64) for o in range(PASSES)]
         slot_scales = keep.tile([P, SLOTS], U8, name="slot_scales", align_bytes=64)
-        gate_rows = keep.tile([P, C], F32, name="gate_rows")
+        gate_row = keep.tile([P, GATE_ROW], F32, name="gate_row")
         gate_cols = keep.tile([P, E], F32, name="gate_cols")
         gates = keep.tile([P, SLOTS], F32, name="gates")
         identity = keep.tile([P, P], F32, name="identity")
         routed = [keep.tile([P, T], F32, name="routed%d" % b) for b in range(BLOCKS)]
         resid = [keep.tile([P, T], F32, name="resid%d" % b) for b in range(BLOCKS)]
         raw = [keep.tile([P, PASSES, PACK, N], F32, name="raw%d" % e) for e in range(E)]
-        rounded = [[keep.tile([P, len(call) * PASSES * K_PASS], BF16, name="rounded%d_%d" % (s, i), align_bytes=64)
-                    for i, call in enumerate(CALLS)] for s in range(CODES_DEPTH)]
+        rounded = [[keep.tile([P, len(layout) * K_PASS], BF16, name="rounded%d_%d" % (s, i), align_bytes=64)
+                    for i, layout in enumerate(LAYOUTS)] for s in range(CODES_DEPTH)]
 
-        def pieces(e, b):
-            i, j = PLACE[e % 2, b]
-            return rounded[e // 2 % CODES_DEPTH][i][:, j * PASSES * K_PASS:(j + 1) * PASSES * K_PASS]
+        def pieces(e, b, o, count):
+            i, j = PLACE[e % 2, b, o]
+            return rounded[e // 2 % CODES_DEPTH][i][:, j * K_PASS:(j + count) * K_PASS]
 
         def load_w(e, o):
             nc.sync.dma_start(out=raw[e][:, o], in_=w[e, o * K_PASS:(o + 1) * K_PASS, :].rearrange("(p t) n -> p t n", t=PACK))
@@ -72,19 +75,21 @@ def tile_moe_res_lin_none_kernel(tc, x_words, x_scales, xr, w, gate, offs, out):
 
         nc.vector.memset(token_scales[:].bitcast(I32), 0)
         nc.sync.dma_start(offsets[:], offs)
-        nc.sync.dma_start(out=gate_rows[:], in_=gate[0:P // E, :].rearrange("r (e c) -> (r e) c", c=C))
-        for quad in range(P // QUADRANT):
+        for quad in (0, 2, 1, 3):
             rows = slice(QUADRANT * quad, QUADRANT * quad + SCALE_ROWS * PASSES)
             nc.sync.dma_start(out=landed_scales[rows, :].bitcast(I32),
                               in_=x_scales[:, SCALE_ROWS * quad:SCALE_ROWS * (quad + 1), :].bitcast(I32))
             nc.vector.tensor_copy(token_scales[rows, :].bitcast(I32), landed_scales[rows, :].bitcast(I32))
 
         load_x(0)
+        nc.sync.dma_start(out=gate_row[:], in_=gate[0, :].rearrange("(p i) -> p i", i=GATE_ROW))
         load_w(0, 0)
         load_x(1)
         for e in range(E):
-            for o in range(PASSES):
-                if (e, o) != (0, 0):
+            if e % 2 == 0 and e > 0:
+                nc.sync.dma_start(out=raw[e][:], in_=w[e].rearrange("(o p t) n -> p o t n", o=PASSES, t=PACK))
+            else:
+                for o in range(1 if e == 0 else 0, PASSES):
                     load_w(e, o)
         for b in range(BLOCKS):
             nc.sync.dma_start(out=resid[b][:], in_=xr[b * P:(b + 1) * P, :])
@@ -97,52 +102,50 @@ def tile_moe_res_lin_none_kernel(tc, x_words, x_scales, xr, w, gate, offs, out):
 
         make_identity(nc, identity[:])
         per_bank = BANK // P
-        columns = psum.tile([P, P], F32, name="back1")
-        nc.tensor.transpose(columns[:], gate_rows[:], identity[:])
-        nc.scalar.activation(out=gate_cols[:], in_=columns[:, 0:E], func=COPY)
-        for h in range(E // per_bank):
+        for h in range(GATE_ROW // per_bank):
             spread = psum.tile([P, per_bank, P], F32, name="bank%d" % h)
             for i in range(per_bank):
+                column = h * per_bank + i
+                nc.tensor.transpose(spread[:, i, :], gate_row[:, column:column + 1].to_broadcast([P, P]), identity[:])
+            nc.scalar.copy(out=gates[:].rearrange("p (s i) -> p s i", i=GATE_ROW)[:, :, h * per_bank:(h + 1) * per_bank],
+                           in_=spread[:].rearrange("p i s -> p s i"))
+        for h in range(E // per_bank):
+            columns = psum.tile([P, per_bank, P], F32, name="back%d" % (h + 1))
+            for i in range(per_bank):
                 e = h * per_bank + i
-                nc.tensor.transpose(spread[:, i, :], gate_cols[:, e:e + 1].to_broadcast([P, P]), identity[:])
-            nc.scalar.copy(out=gates[:, h * BANK:(h + 1) * BANK], in_=spread[:].rearrange("p i s -> p (i s)"))
+                nc.tensor.transpose(columns[:, i, :], gates[:, e * C:(e + 1) * C], identity[:])
+            nc.scalar.activation(out=gate_cols[:, h * per_bank:(h + 1) * per_bank], in_=columns[:, :, 0], func=COPY)
 
         nc.vector.tensor_copy(slot_scales[:], token_scales[:].indirect(offsets[:]))
         for o in range(PASSES):
             nc.vector.tensor_copy(slot_words[o][:], token_words[o][:].bitcast(U32).indirect(offsets[:]))
 
-        def interleave(engine_copy, e, o, b):
+        def interleave(engine_copy, e, o, b, count=1):
             engine_copy(
-                out=pieces(e, b)[:, o * K_PASS:(o + 1) * K_PASS].rearrange("p (c i t) -> p c t i", i=RUN, t=PACK),
-                in_=raw[e][:, o, :, b * P:(b + 1) * P].rearrange("p t (c i) -> p c t i", i=RUN),
+                out=pieces(e, b, o, count).rearrange("p (c i t) -> p c t i", i=RUN, t=PACK),
+                in_=raw[e][:, o, :, b * P:(b + count) * P].rearrange("p t (c i) -> p c t i", i=RUN),
             )
 
         def interleave_on_gpsimd(e, b):
             nc.gpsimd.tensor_scalar(
-                out=pieces(e, b).rearrange("p (o n t) -> p o n t", o=PASSES, t=PACK),
+                out=pieces(e, b, 0, PASSES).rearrange("p (o n t) -> p o n t", o=PASSES, t=PACK),
                 in0=raw[e][:, :, :, b * P:(b + 1) * P].rearrange("p o t n -> p o n t"),
                 scalar1=1.0, scalar2=0.0, op0=MULT, op1=ADD)
 
-        made = {}
+        def quantise(q, tile, lo, hi):
+            codes, scales = made[tile]
+            nc.vector.quantize_mx(out=codes[:, lo * P:hi * P].bitcast(FP8X4), scales=scales[:, lo * P:hi * P],
+                                  in_=rounded[q % CODES_DEPTH][tile][:, lo * K_PASS:hi * K_PASS])
 
-        def quantise_and_multiply(q, i, acc):
-            width = len(CALLS[i]) * PASSES * P
-            codes = ring.tile([P, width], U32, name="codes%d" % i, align_bytes=64)
-            scales = ring.tile([P, width], U8, name="scales%d" % i, align_bytes=64)
-            nc.vector.quantize_mx(out=codes[:].bitcast(FP8X4), scales=scales[:], in_=rounded[q % CODES_DEPTH][i][:])
-            for j, (h, b) in enumerate(CALLS[i]):
-                made[h, b] = (codes, scales, j)
-            for h, b in PRODUCTS[i]:
-                multiply(*made[h, b], 2 * q + h, acc[b], b > 0)
-
-        def multiply(codes, scales, j, e, acc, tokens_stationary):
+        def multiply(e, b, acc, passes=range(PASSES)):
             slots = slice(e * C, (e + 1) * C)
-            for o in range(PASSES):
-                w_cols = slice((j * PASSES + o) * P, (j * PASSES + o + 1) * P)
-                weights = (codes[:, w_cols].bitcast(FP8X4), scales[:, w_cols])
+            for o in passes:
+                tile, j = PLACE[e % 2, b, o]
+                codes, scales = made[tile]
+                weights = (codes[:, j * P:(j + 1) * P].bitcast(FP8X4), scales[:, j * P:(j + 1) * P])
                 tokens = (slot_words[o][:, slots].bitcast(FP8X4), slot_scales[SCALE_ROWS * o:P, slots])
-                fixed, moving = (tokens, weights) if tokens_stationary else (weights, tokens)
-                nc.tensor.matmul_mx(out=acc[:, (e % 2) * C:(e % 2 + 1) * C], lhsT=fixed[0], lhsT_scale=fixed[1],
+                fixed, moving = (tokens, weights) if b > 0 else (weights, tokens)
+                nc.tensor.matmul_mx(out=acc[b][:, (e % 2) * C:(e % 2 + 1) * C], lhsT=fixed[0], lhsT_scale=fixed[1],
                                     rhs=moving[0], rhs_scale=moving[1], start=(o == 0), stop=(o == PASSES - 1))
 
         def window(q, b):
@@ -157,6 +160,8 @@ def tile_moe_res_lin_none_kernel(tc, x_words, x_scales, xr, w, gate, offs, out):
         last = PAIRS - 1
         for q in range(PAIRS):
             first, second = 2 * q, 2 * q + 1
+            made = [(ring.tile([P, len(layout) * P], U32, name="codes%d" % i, align_bytes=64),
+                     ring.tile([P, len(layout) * P], U8, name="scales%d" % i, align_bytes=64)) for i, layout in enumerate(LAYOUTS)]
             acc = [psum.tile([P, PAIR], F32, name="acc%d" % b) for b in range(BLOCKS)]
             back = {b: psum.tile([P, PAIR], F32, name="back%d" % b) for b in range(1, BLOCKS)}
             gated = {b: ring.tile([P, PAIR], F32, name="gated%d" % b) for b in range(1, BLOCKS)}
@@ -164,20 +169,37 @@ def tile_moe_res_lin_none_kernel(tc, x_words, x_scales, xr, w, gate, offs, out):
                 for o in range(PASSES):
                     for b in range(BLOCKS):
                         interleave(nc.scalar.copy, first, o, b)
+                quantise(q, 0, 0, 4)
+                quantise(q, 2, 0, 2)
+                interleave(nc.scalar.copy, second, 0, 0, 2)
+                interleave(nc.vector.tensor_copy, second, 0, LAST_BLOCK)
+                quantise(q, 1, 1, 3)
+                quantise(q, 2, 2, 3)
+                for b in range(BLOCKS):
+                    multiply(first, b, acc)
+                    multiply(second, b, acc, (0,))
+                for b in range(BLOCKS):
+                    interleave(nc.scalar.copy if b == 1 else nc.vector.tensor_copy, second, 1, b)
+                    tile, j = PLACE[1, b, 1]
+                    quantise(q, tile, j, j + 1)
+                    multiply(second, b, acc, (1,))
             else:
-                nc.scalar.copy(out=pieces(first, 0).rearrange("p (o c i t) -> p o c t i", o=PASSES, i=RUN, t=PACK),
+                nc.scalar.copy(out=pieces(first, 0, 0, PASSES).rearrange("p (o c i t) -> p o c t i", o=PASSES, i=RUN, t=PACK),
                                in_=raw[first][:, :, :, 0:P].rearrange("p o t (c i) -> p o c t i", i=RUN))
                 interleave_on_gpsimd(first, 2)
                 interleave_on_gpsimd(first, 1)
-            quantise_and_multiply(q, 0, acc)
-            for o in range(PASSES):
+                quantise(q, *CALLS[0])
+                multiply(first, 0, acc)
+                interleave(nc.scalar.copy, second, 0, 0, 2)
+                interleave(nc.scalar.copy, second, 0, LAST_BLOCK)
                 for b in range(BLOCKS):
-                    interleave(nc.vector.tensor_copy if q == 0 and (o, b) in ((0, LAST_BLOCK), (1, 0)) else nc.scalar.copy, second, o, b)
-                    if o == PASSES - 1:
-                        quantise_and_multiply(q, b + 1, acc)
+                    interleave(nc.scalar.copy, second, 1, b)
+                    quantise(q, *CALLS[b + 1])
+                    for e in ((second,), (second, first), (first, second))[b]:
+                        multiply(e, b, acc)
             for b in range(BLOCKS):
                 if b == 0 and q < last:
-                    values = pieces(first + 2, LAST_BLOCK)[:, 0:2 * PAIR].bitcast(F32)
+                    values = pieces(first + 2, LAST_BLOCK, 0, 1).bitcast(F32)
                 else:
                     values = ring.tile([P, PAIR], F32, name="sums%d" % b)[:]
                 if b == 0:

@@ -211,10 +211,11 @@ def tile_moe_res_lin_none_kernel(tc, x_words, x_scales, xr, w, gate, offs, out):
                     nc.scalar.copy(out=values, in_=back[b][:])
                     nc.vector.tensor_copy(window(q, b), values)
 
-        def add_and_store(engine, b, lo, hi, total):
-            tokens = slice(lo, hi)
-            engine.tensor_tensor(total, resid[b][:, tokens], routed[b][:, tokens], ADD)
-            nc.sync.dma_start(out=out[b * P:(b + 1) * P, tokens], in_=total)
+        def add(engine, b, lo, hi, total):
+            engine.tensor_tensor(total, resid[b][:, lo:hi], routed[b][:, lo:hi], ADD)
+
+        def store(b, lo, hi, total):
+            nc.sync.dma_start(out=out[b * P:(b + 1) * P, lo:hi], in_=total)
 
         turns = [(0, 2), (0, 3), (1, 2), (1, 3)]
         turned = [keep.tile([P, 2, per_bank, P], F32, name="turned%d" % j) for j in range(len(turns) // 2)]
@@ -236,10 +237,13 @@ def tile_moe_res_lin_none_kernel(tc, x_words, x_scales, xr, w, gate, offs, out):
                 nc.tensor.transpose(back[:, i, :], turned[j // 2][:, j % 2, i, :], identity[:])
             tokens = slice(c * BANK, (c + 1) * BANK)
             nc.scalar.copy(out=resid[b][:, tokens], in_=back[:].rearrange("p i s -> p (i s)"))
-            nc.sync.dma_start(out=out[b * P:(b + 1) * P, tokens], in_=resid[b][:, tokens])
+            if b == 0:
+                store(b, tokens.start, tokens.stop, resid[b][:, tokens])
 
-        for c in range(2):
-            add_and_store(nc.gpsimd, 0, c * BANK, (c + 1) * BANK, resid[0][:, c * BANK:(c + 1) * BANK])
+        half = 2 * BANK
+        for lo in range(0, half, BANK):
+            add(nc.gpsimd, 0, lo, lo + BANK, resid[0][:, lo:lo + BANK])
+            store(0, lo, lo + BANK, resid[0][:, lo:lo + BANK])
         turn(0)
         turn(1)
         turn_back(0)
@@ -248,7 +252,11 @@ def tile_moe_res_lin_none_kernel(tc, x_words, x_scales, xr, w, gate, offs, out):
         turn(3)
         turn_back(2)
         turn_back(3)
-        for c in range(2):
-            add_and_store(nc.vector, 1, c * BANK, (c + 1) * BANK, turned[0][:, c].rearrange("p i s -> p (i s)"))
-        for c in range(T // BANK):
-            add_and_store(nc.vector, LAST_BLOCK, c * BANK, (c + 1) * BANK, resid[LAST_BLOCK][:, c * BANK:(c + 1) * BANK])
+        store(1, half, T, resid[1][:, half:T])
+        spent = turned[0][:].rearrange("p j i s -> p (j i s)")
+        for lo in range(0, half, BANK):
+            add(nc.vector, 1, lo, lo + BANK, spent[:, lo:lo + BANK])
+            store(1, lo, lo + BANK, spent[:, lo:lo + BANK])
+        for lo, hi in ((0, BANK), (BANK, half), (half, T)):
+            add(nc.vector, LAST_BLOCK, lo, hi, resid[LAST_BLOCK][:, lo:hi])
+            store(LAST_BLOCK, lo, hi, resid[LAST_BLOCK][:, lo:hi])

@@ -22,7 +22,6 @@ PACK = 4
 K_PASS = P * PACK
 PASSES = K // K_PASS
 BLOCKS = N // P
-LAST_BLOCK = BLOCKS - 1
 SLOTS = E * C
 PAIRS = E // 2
 PAIR = 2 * C
@@ -30,22 +29,18 @@ LIST_ROWS = 16
 QUADRANT = 32
 SCALE_ROWS = 4
 RUN = 4
-CODES_DEPTH = 2
-LAYOUTS = (((0, 0, 0), (0, 0, 1), (0, 1, 0), (0, 1, 1)),
-           ((1, 0, 1), (1, 0, 0), (1, 1, 0), (1, 1, 1)),
-           ((0, 2, 0), (0, 2, 1), (1, 2, 0), (1, 2, 1)))
-CALLS = ((0, 0, 4), (1, 0, 2), (1, 2, 4), (2, 0, 4))
-PLACE = {piece: (i, j) for i, layout in enumerate(LAYOUTS) for j, piece in enumerate(layout)}
+DEPTH = 2
 GATE_ROW = SLOTS // P
 BANK = 512
+HALF = T // 2
 
 
 def tile_moe_res_lin_none_kernel(tc, x_words, x_scales, xr, w, gate, offs, out):
     nc = tc.nc
     with ExitStack() as ctx:
         keep = ctx.enter_context(tc.tile_pool(name="keep", bufs=1))
-        ring = ctx.enter_context(tc.tile_pool(name="ring", bufs=CODES_DEPTH))
-        psum = ctx.enter_context(tc.psum_pool(name="psum", bufs=1))
+        ring = ctx.enter_context(tc.tile_pool(name="ring", bufs=DEPTH))
+        psum = ctx.enter_context(tc.psum_pool(name="psum", bufs=DEPTH))
 
         offsets = keep.tile([P, SLOTS // LIST_ROWS], U16, name="offsets")
         landed_scales = keep.tile([P, T], U8, name="landed_scales")
@@ -54,21 +49,14 @@ def tile_moe_res_lin_none_kernel(tc, x_words, x_scales, xr, w, gate, offs, out):
         slot_words = [keep.tile([P, SLOTS], U32, name="slot_words%d" % o, align_bytes=64) for o in range(PASSES)]
         slot_scales = keep.tile([P, SLOTS], U8, name="slot_scales", align_bytes=64)
         gate_row = keep.tile([P, GATE_ROW], F32, name="gate_row")
-        gate_cols = keep.tile([P, E], F32, name="gate_cols")
         gates = keep.tile([P, SLOTS], F32, name="gates")
         identity = keep.tile([P, P], F32, name="identity")
         routed = [keep.tile([P, T], F32, name="routed%d" % b) for b in range(BLOCKS)]
         resid = [keep.tile([P, T], F32, name="resid%d" % b) for b in range(BLOCKS)]
-        raw = [keep.tile([P, PASSES, PACK, N], F32, name="raw%d" % e) for e in range(E)]
-        rounded = [[keep.tile([P, len(layout) * K_PASS], BF16, name="rounded%d_%d" % (s, i), align_bytes=64)
-                    for i, layout in enumerate(LAYOUTS)] for s in range(CODES_DEPTH)]
-
-        def pieces(e, b, o, count):
-            i, j = PLACE[e % 2, b, o]
-            return rounded[e // 2 % CODES_DEPTH][i][:, j * K_PASS:(j + count) * K_PASS]
+        raw = [[keep.tile([P, PACK, N], F32, name="raw%d_%d" % (e, o)) for o in range(PASSES)] for e in range(E)]
 
         def load_w(e, o):
-            nc.sync.dma_start(out=raw[e][:, o], in_=w[e, o * K_PASS:(o + 1) * K_PASS, :].rearrange("(p t) n -> p t n", t=PACK))
+            nc.sync.dma_start(out=raw[e][o][:], in_=w[e, o * K_PASS:(o + 1) * K_PASS, :].rearrange("(p t) n -> p t n", t=PACK))
 
         def load_x(o):
             nc.sync.dma_start(out=token_words[o][:], in_=x_words[o].rearrange("p t r -> p (t r)").bitcast(I32))
@@ -86,177 +74,67 @@ def tile_moe_res_lin_none_kernel(tc, x_words, x_scales, xr, w, gate, offs, out):
         load_w(0, 0)
         load_x(1)
         for e in range(E):
-            if e % 2 == 0 and e > 0:
-                nc.sync.dma_start(out=raw[e][:], in_=w[e].rearrange("(o p t) n -> p o t n", o=PASSES, t=PACK))
-            else:
-                for o in range(1 if e == 0 else 0, PASSES):
-                    load_w(e, o)
+            for o in range(1 if e == 0 else 0, PASSES):
+                load_w(e, o)
         for b in range(BLOCKS):
             nc.sync.dma_start(out=resid[b][:], in_=xr[b * P:(b + 1) * P, :])
 
         zeros = keep.tile([P, P], F32, name="zeros")
         nc.vector.memset(zeros[:], 0.0)
         for b in range(BLOCKS):
-            copy = nc.scalar.copy if b == LAST_BLOCK else nc.vector.tensor_copy
+            copy = nc.vector.tensor_copy if b == 0 else nc.scalar.copy
             copy(out=routed[b][:].rearrange("p (r c) -> p r c", c=P), in_=zeros[:].unsqueeze(1).to_broadcast([P, T // P, P]))
 
         make_identity(nc, identity[:])
         per_bank = BANK // P
         for h in range(GATE_ROW // per_bank):
-            spread = psum.tile([P, per_bank, P], F32, name="bank%d" % h)
+            spread = psum.tile([P, per_bank, P], F32, name="spread")
             for i in range(per_bank):
                 column = h * per_bank + i
                 nc.tensor.transpose(spread[:, i, :], gate_row[:, column:column + 1].to_broadcast([P, P]), identity[:])
             nc.scalar.copy(out=gates[:].rearrange("p (s i) -> p s i", i=GATE_ROW)[:, :, h * per_bank:(h + 1) * per_bank],
                            in_=spread[:].rearrange("p i s -> p s i"))
-        for h in range(E // per_bank):
-            columns = psum.tile([P, per_bank, P], F32, name="back%d" % (h + 1))
-            for i in range(per_bank):
-                e = h * per_bank + i
-                nc.tensor.transpose(columns[:, i, :], gates[:, e * C:(e + 1) * C], identity[:])
-            nc.scalar.activation(out=gate_cols[:, h * per_bank:(h + 1) * per_bank], in_=columns[:, :, 0], func=COPY)
 
         nc.vector.tensor_copy(slot_scales[:], token_scales[:].indirect(offsets[:]))
         for o in range(PASSES):
             nc.vector.tensor_copy(slot_words[o][:], token_words[o][:].bitcast(U32).indirect(offsets[:]))
 
-        def interleave(engine_copy, e, o, b, count=1):
-            engine_copy(
-                out=pieces(e, b, o, count).rearrange("p (c i t) -> p c t i", i=RUN, t=PACK),
-                in_=raw[e][:, o, :, b * P:(b + count) * P].rearrange("p t (c i) -> p c t i", i=RUN),
-            )
-
-        def interleave_on_gpsimd(e, b):
-            nc.gpsimd.tensor_scalar(
-                out=pieces(e, b, 0, PASSES).rearrange("p (o n t) -> p o n t", o=PASSES, t=PACK),
-                in0=raw[e][:, :, :, b * P:(b + 1) * P].rearrange("p o t n -> p o n t"),
-                scalar1=1.0, scalar2=0.0, op0=MULT, op1=ADD)
-
-        def quantise(q, tile, lo, hi):
-            codes, scales = made[tile]
-            nc.vector.quantize_mx(out=codes[:, lo * P:hi * P].bitcast(FP8X4), scales=scales[:, lo * P:hi * P],
-                                  in_=rounded[q % CODES_DEPTH][tile][:, lo * K_PASS:hi * K_PASS])
-
-        def multiply(e, b, acc, passes=range(PASSES)):
-            slots = slice(e * C, (e + 1) * C)
-            for o in passes:
-                tile, j = PLACE[e % 2, b, o]
-                codes, scales = made[tile]
-                weights = (codes[:, j * P:(j + 1) * P].bitcast(FP8X4), scales[:, j * P:(j + 1) * P])
-                tokens = (slot_words[o][:, slots].bitcast(FP8X4), slot_scales[SCALE_ROWS * o:P, slots])
-                fixed, moving = (tokens, weights) if b > 0 else (weights, tokens)
-                nc.tensor.matmul_mx(out=acc[b][:, (e % 2) * C:(e % 2 + 1) * C], lhsT=fixed[0], lhsT_scale=fixed[1],
-                                    rhs=moving[0], rhs_scale=moving[1], start=(o == 0), stop=(o == PASSES - 1))
-
-        def window(q, b):
-            entries = slice(q * PAIR // LIST_ROWS, (q + 1) * PAIR // LIST_ROWS)
-            return routed[b][:].indirect(offsets[:, entries])
-
-        def gate_and_turn(e, acc, gated, back):
-            cols = slice((e % 2) * C, (e % 2 + 1) * C)
-            nc.scalar.activation(out=gated[:, cols], in_=acc[:, cols], func=COPY, scale=gate_cols[:, e:e + 1])
-            nc.tensor.transpose(back[:, cols], gated[:, cols], identity[:])
-
-        last = PAIRS - 1
         for q in range(PAIRS):
-            first, second = 2 * q, 2 * q + 1
-            made = [(ring.tile([P, len(layout) * P], U32, name="codes%d" % i, align_bytes=64),
-                     ring.tile([P, len(layout) * P], U8, name="scales%d" % i, align_bytes=64)) for i, layout in enumerate(LAYOUTS)]
             acc = [psum.tile([P, PAIR], F32, name="acc%d" % b) for b in range(BLOCKS)]
-            back = {b: psum.tile([P, PAIR], F32, name="back%d" % b) for b in range(1, BLOCKS)}
-            gated = {b: ring.tile([P, PAIR], F32, name="gated%d" % b) for b in range(1, BLOCKS)}
-            if q == 0:
+            for side in range(2):
+                e = 2 * q + side
+                slots = slice(e * C, (e + 1) * C)
+                made = []
                 for o in range(PASSES):
-                    for b in range(BLOCKS):
-                        interleave(nc.scalar.copy, first, o, b)
-                quantise(q, 0, 0, 4)
-                quantise(q, 2, 0, 2)
-                interleave(nc.scalar.copy, second, 0, 0, 2)
-                interleave(nc.vector.tensor_copy, second, 0, LAST_BLOCK)
-                quantise(q, 1, 1, 3)
-                quantise(q, 2, 2, 3)
+                    rounded = ring.tile([P, N * PACK], BF16, name="rounded%d_%d" % (side, o), align_bytes=64)
+                    codes = ring.tile([P, N], U32, name="codes%d_%d" % (side, o), align_bytes=64)
+                    scales = ring.tile([P, N], U8, name="scales%d_%d" % (side, o), align_bytes=64)
+                    made.append((codes, scales))
+                    on_scalar = (q == 0 and (side, o) != (1, 1)) or (side, o) == (0, 0)
+                    cuts = ((0, 2 * P), (2 * P, N))
+                    for lo, hi in cuts:
+                        copy = nc.scalar.copy if on_scalar and (q == 0 or lo == 0) else nc.vector.tensor_copy
+                        copy(out=rounded[:, lo * PACK:hi * PACK].rearrange("p (c i t) -> p c t i", i=RUN, t=PACK),
+                             in_=raw[e][o][:, :, lo:hi].rearrange("p t (c i) -> p c t i", i=RUN))
+                    for lo, hi in cuts:
+                        nc.vector.quantize_mx(out=codes[:, lo:hi].bitcast(FP8X4), scales=scales[:, lo:hi],
+                                              in_=rounded[:, lo * PACK:hi * PACK])
                 for b in range(BLOCKS):
-                    multiply(first, b, acc)
-                    multiply(second, b, acc, (0,))
-                for b in range(BLOCKS):
-                    interleave(nc.scalar.copy if b == 1 else nc.vector.tensor_copy, second, 1, b)
-                    tile, j = PLACE[1, b, 1]
-                    quantise(q, tile, j, j + 1)
-                    multiply(second, b, acc, (1,))
-            else:
-                nc.scalar.copy(out=pieces(first, 0, 0, PASSES).rearrange("p (o c i t) -> p o c t i", o=PASSES, i=RUN, t=PACK),
-                               in_=raw[first][:, :, :, 0:P].rearrange("p o t (c i) -> p o c t i", i=RUN))
-                interleave_on_gpsimd(first, 2)
-                interleave_on_gpsimd(first, 1)
-                quantise(q, *CALLS[0])
-                multiply(first, 0, acc)
-                interleave(nc.scalar.copy, second, 0, 0, 2)
-                interleave(nc.scalar.copy, second, 0, LAST_BLOCK)
-                for b in range(BLOCKS):
-                    interleave(nc.scalar.copy, second, 1, b)
-                    quantise(q, *CALLS[b + 1])
-                    for e in ((second,), (second, first), (first, second))[b]:
-                        multiply(e, b, acc)
+                    cols = slice(b * P, (b + 1) * P)
+                    for o in range(PASSES):
+                        codes, scales = made[o]
+                        nc.tensor.matmul_mx(out=acc[b][:, side * C:(side + 1) * C],
+                                            lhsT=codes[:, cols].bitcast(FP8X4), lhsT_scale=scales[:, cols],
+                                            rhs=slot_words[o][:, slots].bitcast(FP8X4), rhs_scale=slot_scales[SCALE_ROWS * o:P, slots],
+                                            start=(o == 0), stop=(o == PASSES - 1))
+            entries = slice(q * PAIR // LIST_ROWS, (q + 1) * PAIR // LIST_ROWS)
             for b in range(BLOCKS):
-                if b == 0 and q < last:
-                    values = pieces(first + 2, LAST_BLOCK, 0, 1).bitcast(F32)
-                else:
-                    values = ring.tile([P, PAIR], F32, name="sums%d" % b)[:]
-                if b == 0:
-                    nc.scalar.copy(out=values, in_=acc[b][:])
-                    nc.vector.tensor_tensor(window(q, b), values, gates[:, q * PAIR:(q + 1) * PAIR], MULT)
-                else:
-                    for e in (first, second):
-                        gate_and_turn(e, acc[b], gated[b], back[b])
-                    nc.scalar.copy(out=values, in_=back[b][:])
-                    nc.vector.tensor_copy(window(q, b), values)
+                gated = ring.tile([P, PAIR], F32, name="gated%d" % b)
+                nc.vector.tensor_tensor(gated[:], acc[b][:], gates[:, q * PAIR:(q + 1) * PAIR], MULT)
+                nc.scalar.activation(out=routed[b][:].indirect(offsets[:, entries]), in_=gated[:], func=COPY)
 
-        def add(engine, b, lo, hi, total):
-            engine.tensor_tensor(total, resid[b][:, lo:hi], routed[b][:, lo:hi], ADD)
-
-        def store(b, lo, hi, total):
-            nc.sync.dma_start(out=out[b * P:(b + 1) * P, lo:hi], in_=total)
-
-        turns = [(0, 2), (0, 3), (1, 2), (1, 3)]
-        turned = [keep.tile([P, 2, per_bank, P], F32, name="turned%d" % j) for j in range(len(turns) // 2)]
-
-        def turn(j):
-            b, c = turns[j]
-            total = psum.tile([P, per_bank, P], F32, name="bank%d" % j if j < len(turns) - 1 else "acc0")
-            for source in (resid[b], routed[b]):
-                for i in range(per_bank):
-                    cols = slice(c * BANK + i * P, c * BANK + (i + 1) * P)
-                    nc.tensor.matmul(total[:, i, :], source[:, cols], identity[:], is_transpose=True,
-                                     start=(source is resid[b] and i == 0), stop=(source is routed[b] and i == per_bank - 1))
-            nc.scalar.copy(out=turned[j // 2][:, j % 2], in_=total[:])
-
-        def turn_back(j):
-            b, c = turns[j]
-            back = psum.tile([P, per_bank, P], F32, name="bank%d" % (j - 1) if j > 0 else "acc1")
-            for i in range(per_bank):
-                nc.tensor.transpose(back[:, i, :], turned[j // 2][:, j % 2, i, :], identity[:])
-            tokens = slice(c * BANK, (c + 1) * BANK)
-            nc.scalar.copy(out=resid[b][:, tokens], in_=back[:].rearrange("p i s -> p (i s)"))
-            if b == 0:
-                store(b, tokens.start, tokens.stop, resid[b][:, tokens])
-
-        half = 2 * BANK
-        for lo in range(0, half, BANK):
-            add(nc.gpsimd, 0, lo, lo + BANK, resid[0][:, lo:lo + BANK])
-            store(0, lo, lo + BANK, resid[0][:, lo:lo + BANK])
-        turn(0)
-        turn(1)
-        turn_back(0)
-        turn(2)
-        turn_back(1)
-        turn(3)
-        turn_back(2)
-        turn_back(3)
-        store(1, half, T, resid[1][:, half:T])
-        spent = turned[0][:].rearrange("p j i s -> p (j i s)")
-        for lo in range(0, half, BANK):
-            add(nc.vector, 1, lo, lo + BANK, spent[:, lo:lo + BANK])
-            store(1, lo, lo + BANK, spent[:, lo:lo + BANK])
-        for lo, hi in ((0, BANK), (BANK, half), (half, T)):
-            add(nc.vector, LAST_BLOCK, lo, hi, resid[LAST_BLOCK][:, lo:hi])
-            store(LAST_BLOCK, lo, hi, resid[LAST_BLOCK][:, lo:hi])
+        for b in range(BLOCKS):
+            for lo in range(0, T, HALF):
+                tokens = slice(lo, lo + HALF)
+                nc.vector.tensor_tensor(resid[b][:, tokens], resid[b][:, tokens], routed[b][:, tokens], ADD)
+                nc.sync.dma_start(out=out[b * P:(b + 1) * P, tokens], in_=resid[b][:, tokens])

@@ -43,7 +43,6 @@ def tile_moe_res_lin_none_kernel(tc, x_words, x_scales, xr, w, gate, offs, out):
         psum = ctx.enter_context(tc.psum_pool(name="psum", bufs=DEPTH))
 
         offsets = keep.tile([P, SLOTS // LIST_ROWS], U16, name="offsets")
-        landed_scales = keep.tile([P, T], U8, name="landed_scales")
         token_scales = keep.tile([P, T], U8, name="token_scales")
         token_words = [keep.tile([P, T], I32, name="token_words%d" % o) for o in range(PASSES)]
         slot_words = [keep.tile([P, SLOTS], U32, name="slot_words%d" % o, align_bytes=64) for o in range(PASSES)]
@@ -61,20 +60,17 @@ def tile_moe_res_lin_none_kernel(tc, x_words, x_scales, xr, w, gate, offs, out):
         def load_x(o):
             nc.sync.dma_start(out=token_words[o][:], in_=x_words[o].rearrange("p t r -> p (t r)").bitcast(I32))
 
-        nc.vector.memset(token_scales[:].bitcast(I32), 0)
+        nc.gpsimd.memset(token_scales[:].bitcast(I32), 0)
         nc.sync.dma_start(offsets[:], offs)
+        load_x(0)
         for quad in (0, 2, 1, 3):
             rows = slice(QUADRANT * quad, QUADRANT * quad + SCALE_ROWS * PASSES)
-            nc.sync.dma_start(out=landed_scales[rows, :].bitcast(I32),
+            nc.sync.dma_start(out=token_scales[rows, :].bitcast(I32),
                               in_=x_scales[:, SCALE_ROWS * quad:SCALE_ROWS * (quad + 1), :].bitcast(I32))
-            nc.vector.tensor_copy(token_scales[rows, :].bitcast(I32), landed_scales[rows, :].bitcast(I32))
-
-        load_x(0)
-        nc.sync.dma_start(out=gate_row[:], in_=gate[0, :].rearrange("(p i) -> p i", i=GATE_ROW))
-        load_w(0, 0)
         load_x(1)
+        nc.sync.dma_start(out=gate_row[:], in_=gate[0, :].rearrange("(p i) -> p i", i=GATE_ROW))
         for e in range(E):
-            for o in range(1 if e == 0 else 0, PASSES):
+            for o in range(PASSES):
                 load_w(e, o)
         for b in range(BLOCKS):
             nc.sync.dma_start(out=resid[b][:], in_=xr[b * P:(b + 1) * P, :])
@@ -95,46 +91,69 @@ def tile_moe_res_lin_none_kernel(tc, x_words, x_scales, xr, w, gate, offs, out):
             nc.scalar.copy(out=gates[:].rearrange("p (s i) -> p s i", i=GATE_ROW)[:, :, h * per_bank:(h + 1) * per_bank],
                            in_=spread[:].rearrange("p i s -> p s i"))
 
-        nc.vector.tensor_copy(slot_scales[:], token_scales[:].indirect(offsets[:]))
         for o in range(PASSES):
             nc.vector.tensor_copy(slot_words[o][:], token_words[o][:].bitcast(U32).indirect(offsets[:]))
+            if o == 0:
+                nc.vector.tensor_copy(slot_scales[:], token_scales[:].indirect(offsets[:]))
+
+        def interleave(copy, e, o, lo, hi):
+            copy(out=made[e % 2, o][0][:, lo * PACK:hi * PACK].rearrange("p (c i t) -> p c t i", i=RUN, t=PACK),
+                 in_=raw[e][o][:, :, lo:hi].rearrange("p t (c i) -> p c t i", i=RUN))
+
+        def quantise(e, o, lo, hi):
+            rounded, codes, scales = made[e % 2, o]
+            nc.vector.quantize_mx(out=codes[:, lo:hi].bitcast(FP8X4), scales=scales[:, lo:hi], in_=rounded[:, lo * PACK:hi * PACK])
+
+        def multiply(e, o, b):
+            codes, scales = made[e % 2, o][1:]
+            cols, slots = slice(b * P, (b + 1) * P), slice(e * C, (e + 1) * C)
+            nc.tensor.matmul_mx(out=acc[b][:, (e % 2) * C:(e % 2 + 1) * C],
+                                lhsT=codes[:, cols].bitcast(FP8X4), lhsT_scale=scales[:, cols],
+                                rhs=slot_words[o][:, slots].bitcast(FP8X4), rhs_scale=slot_scales[SCALE_ROWS * o:P, slots],
+                                start=(o == 0), stop=(o == PASSES - 1))
+
+        def scatter(q, b):
+            entries = slice(q * PAIR // LIST_ROWS, (q + 1) * PAIR // LIST_ROWS)
+            gated = ring.tile([P, PAIR], F32, name="gated%d" % b)
+            nc.vector.tensor_tensor(gated[:], acc[b][:], gates[:, q * PAIR:(q + 1) * PAIR], MULT)
+            nc.scalar.activation(out=routed[b][:].indirect(offsets[:, entries]), in_=gated[:], func=COPY)
 
         for q in range(PAIRS):
             acc = [psum.tile([P, PAIR], F32, name="acc%d" % b) for b in range(BLOCKS)]
-            for side in range(2):
-                e = 2 * q + side
-                slots = slice(e * C, (e + 1) * C)
-                made = []
+            made = {(side, o): (ring.tile([P, N * PACK], BF16, name="rounded%d_%d" % (side, o), align_bytes=64),
+                                ring.tile([P, N], U32, name="codes%d_%d" % (side, o), align_bytes=64),
+                                ring.tile([P, N], U8, name="scales%d_%d" % (side, o), align_bytes=64))
+                    for side in range(2) for o in range(PASSES)}
+            for e in (2 * q, 2 * q + 1):
                 for o in range(PASSES):
-                    rounded = ring.tile([P, N * PACK], BF16, name="rounded%d_%d" % (side, o), align_bytes=64)
-                    codes = ring.tile([P, N], U32, name="codes%d_%d" % (side, o), align_bytes=64)
-                    scales = ring.tile([P, N], U8, name="scales%d_%d" % (side, o), align_bytes=64)
-                    made.append((codes, scales))
-                    on_scalar = (q == 0 and (side, o) != (1, 1)) or (side, o) == (0, 0)
+                    if (e, o) == (E - 1, PASSES - 1):
+                        continue
                     cuts = ((0, 2 * P), (2 * P, N))
-                    for lo, hi in cuts:
-                        copy = nc.scalar.copy if on_scalar and (q == 0 or lo == 0) else nc.vector.tensor_copy
-                        copy(out=rounded[:, lo * PACK:hi * PACK].rearrange("p (c i t) -> p c t i", i=RUN, t=PACK),
-                             in_=raw[e][o][:, :, lo:hi].rearrange("p t (c i) -> p c t i", i=RUN))
-                    for lo, hi in cuts:
-                        nc.vector.quantize_mx(out=codes[:, lo:hi].bitcast(FP8X4), scales=scales[:, lo:hi],
-                                              in_=rounded[:, lo * PACK:hi * PACK])
+                    on_scalar = cuts if q == 0 and (e, o) != (1, 1) else cuts[:1] if (e % 2, o) == (0, 0) else ()
+                    for cut in cuts:
+                        interleave(nc.scalar.copy if cut in on_scalar else nc.vector.tensor_copy, e, o, *cut)
+                    for cut in cuts:
+                        quantise(e, o, *cut)
+                    for b in range(BLOCKS):
+                        multiply(e, o, b)
+            if q < PAIRS - 1:
                 for b in range(BLOCKS):
-                    cols = slice(b * P, (b + 1) * P)
-                    for o in range(PASSES):
-                        codes, scales = made[o]
-                        nc.tensor.matmul_mx(out=acc[b][:, side * C:(side + 1) * C],
-                                            lhsT=codes[:, cols].bitcast(FP8X4), lhsT_scale=scales[:, cols],
-                                            rhs=slot_words[o][:, slots].bitcast(FP8X4), rhs_scale=slot_scales[SCALE_ROWS * o:P, slots],
-                                            start=(o == 0), stop=(o == PASSES - 1))
-            entries = slice(q * PAIR // LIST_ROWS, (q + 1) * PAIR // LIST_ROWS)
-            for b in range(BLOCKS):
-                gated = ring.tile([P, PAIR], F32, name="gated%d" % b)
-                nc.vector.tensor_tensor(gated[:], acc[b][:], gates[:, q * PAIR:(q + 1) * PAIR], MULT)
-                nc.scalar.activation(out=routed[b][:].indirect(offsets[:, entries]), in_=gated[:], func=COPY)
+                    scatter(q, b)
+            else:
+                e, o = E - 1, PASSES - 1
+                interleave(nc.vector.tensor_copy, e, o, 0, P)
+                for b in range(BLOCKS + 1):
+                    if b + 1 < BLOCKS:
+                        interleave(nc.vector.tensor_copy, e, o, (b + 1) * P, (b + 2) * P)
+                    if b < BLOCKS:
+                        quantise(e, o, b * P, (b + 1) * P)
+                        multiply(e, o, b)
+                    if b > 0:
+                        scatter(q, b - 1)
 
         for b in range(BLOCKS):
-            for lo in range(0, T, HALF):
-                tokens = slice(lo, lo + HALF)
+            cuts = (0, HALF, T) if b < BLOCKS - 1 else (0, HALF, T - HALF // 2, T)
+            for lo, hi in zip(cuts, cuts[1:]):
+                tokens = slice(lo, hi)
                 nc.vector.tensor_tensor(resid[b][:, tokens], resid[b][:, tokens], routed[b][:, tokens], ADD)
                 nc.sync.dma_start(out=out[b * P:(b + 1) * P, tokens], in_=resid[b][:, tokens])

@@ -62,12 +62,11 @@ def tile_moe_res_lin_none_kernel(tc, x_words, x_scales, xr, w, gate, offs, out):
 
         nc.gpsimd.memset(token_scales[:].bitcast(I32), 0)
         nc.sync.dma_start(offsets[:], offs)
-        load_x(0)
-        for quad in (0, 2, 1, 3):
-            rows = slice(QUADRANT * quad, QUADRANT * quad + SCALE_ROWS * PASSES)
-            nc.sync.dma_start(out=token_scales[rows, :].bitcast(I32),
-                              in_=x_scales[:, SCALE_ROWS * quad:SCALE_ROWS * (quad + 1), :].bitcast(I32))
-        load_x(1)
+        for o in range(PASSES):
+            load_x(o)
+            for j in range(SCALE_ROWS):
+                nc.sync.dma_start(out=token_scales[SCALE_ROWS * o + j:P:QUADRANT, :].bitcast(I32),
+                                  in_=x_scales[o, j::SCALE_ROWS, :].bitcast(I32))
         nc.sync.dma_start(out=gate_row[:], in_=gate[0, :].rearrange("(p i) -> p i", i=GATE_ROW))
         for e in range(E):
             for o in range(PASSES):
@@ -93,7 +92,7 @@ def tile_moe_res_lin_none_kernel(tc, x_words, x_scales, xr, w, gate, offs, out):
 
         for o in range(PASSES):
             nc.vector.tensor_copy(slot_words[o][:], token_words[o][:].bitcast(U32).indirect(offsets[:]))
-            if o == 0:
+            if o == PASSES - 1:
                 nc.vector.tensor_copy(slot_scales[:], token_scales[:].indirect(offsets[:]))
 
         def interleave(copy, e, o, lo, hi):

@@ -62,12 +62,12 @@ def tile_moe_res_lin_none_kernel(tc, x_words, x_scales, xr, w, gate, offs, out):
 
         nc.gpsimd.memset(token_scales[:].bitcast(I32), 0)
         nc.sync.dma_start(offsets[:], offs)
+        nc.sync.dma_start(out=gate_row[:], in_=gate[0, :].rearrange("(p i) -> p i", i=GATE_ROW))
         for o in range(PASSES):
             load_x(o)
             for j in range(SCALE_ROWS):
                 nc.sync.dma_start(out=token_scales[SCALE_ROWS * o + j:P:QUADRANT, :].bitcast(I32),
                                   in_=x_scales[o, j::SCALE_ROWS, :].bitcast(I32))
-        nc.sync.dma_start(out=gate_row[:], in_=gate[0, :].rearrange("(p i) -> p i", i=GATE_ROW))
         for e in range(E):
             for o in range(PASSES):
                 load_w(e, o)
@@ -115,7 +115,10 @@ def tile_moe_res_lin_none_kernel(tc, x_words, x_scales, xr, w, gate, offs, out):
             entries = slice(q * PAIR // LIST_ROWS, (q + 1) * PAIR // LIST_ROWS)
             gated = ring.tile([P, PAIR], F32, name="gated%d" % b)
             nc.vector.tensor_tensor(gated[:], acc[b][:], gates[:, q * PAIR:(q + 1) * PAIR], MULT)
-            nc.scalar.activation(out=routed[b][:].indirect(offsets[:, entries]), in_=gated[:], func=COPY)
+            if (q, b) == (PAIRS - 1, 0):
+                nc.vector.tensor_copy(routed[b][:].indirect(offsets[:, entries]), gated[:])
+            else:
+                nc.scalar.activation(out=routed[b][:].indirect(offsets[:, entries]), in_=gated[:], func=COPY)
 
         for q in range(PAIRS):
             acc = [psum.tile([P, PAIR], F32, name="acc%d" % b) for b in range(BLOCKS)]

@@ -103,25 +103,36 @@ def tile_moe_res_lin_none_kernel(tc, x_words, x_scales, xr, w, gate, offs, out):
             rounded, codes, scales = made[e % 2, o]
             nc.vector.quantize_mx(out=codes[:, lo:hi].bitcast(FP8X4), scales=scales[:, lo:hi], in_=rounded[:, lo * PACK:hi * PACK])
 
+        def group(e, b):
+            if b == 0 and e >= E - 4:
+                return (E - 4, E - 1) if e < E - 1 else (E - 1, E)
+            return (e - e % 2, e - e % 2 + 2)
+
         def multiply(e, o, b):
             codes, scales = made[e % 2, o][1:]
+            first, end = group(e, b)
+            if (e, o) == (first, 0):
+                acc[b] = psum.tile([P, (end - first) * C], F32, name="acc%d" % b)
             cols, slots = slice(b * P, (b + 1) * P), slice(e * C, (e + 1) * C)
-            nc.tensor.matmul_mx(out=acc[b][:, (e % 2) * C:(e % 2 + 1) * C],
+            nc.tensor.matmul_mx(out=acc[b][:, (e - first) * C:(e - first + 1) * C],
                                 lhsT=codes[:, cols].bitcast(FP8X4), lhsT_scale=scales[:, cols],
                                 rhs=slot_words[o][:, slots].bitcast(FP8X4), rhs_scale=slot_scales[SCALE_ROWS * o:P, slots],
                                 start=(o == 0), stop=(o == PASSES - 1))
 
-        def scatter(q, b):
-            entries = slice(q * PAIR // LIST_ROWS, (q + 1) * PAIR // LIST_ROWS)
-            gated = ring.tile([P, PAIR], F32, name="gated%d" % b)
-            nc.vector.tensor_tensor(gated[:], acc[b][:], gates[:, q * PAIR:(q + 1) * PAIR], MULT)
-            if (q, b) == (PAIRS - 1, 0):
-                nc.vector.tensor_copy(routed[b][:].indirect(offsets[:, entries]), gated[:])
+        def scatter(e, b):
+            first, end = group(e, b)
+            if e < end - 1:
+                return
+            window = routed[b][:].indirect(offsets[:, first * C // LIST_ROWS:end * C // LIST_ROWS])
+            gated = ring.tile([P, (end - first) * C], F32, name="gated%d" % b)
+            nc.vector.tensor_tensor(gated[:], acc[b][:], gates[:, first * C:end * C], MULT)
+            if end - first == 1:
+                nc.vector.tensor_tensor(window, gated[:], zeros[:], ADD)
             else:
-                nc.scalar.activation(out=routed[b][:].indirect(offsets[:, entries]), in_=gated[:], func=COPY)
+                nc.scalar.activation(out=window, in_=gated[:], func=COPY)
 
+        acc = {}
         for q in range(PAIRS):
-            acc = [psum.tile([P, PAIR], F32, name="acc%d" % b) for b in range(BLOCKS)]
             made = {(side, o): (ring.tile([P, N * PACK], BF16, name="rounded%d_%d" % (side, o), align_bytes=64),
                                 ring.tile([P, N], U32, name="codes%d_%d" % (side, o), align_bytes=64),
                                 ring.tile([P, N], U8, name="scales%d_%d" % (side, o), align_bytes=64))
@@ -138,10 +149,10 @@ def tile_moe_res_lin_none_kernel(tc, x_words, x_scales, xr, w, gate, offs, out):
                         quantise(e, o, *cut)
                     for b in range(BLOCKS):
                         multiply(e, o, b)
-            if q < PAIRS - 1:
-                for b in range(BLOCKS):
-                    scatter(q, b)
-            else:
+                    if o == PASSES - 1:
+                        for b in range(BLOCKS):
+                            scatter(e, b)
+            if q == PAIRS - 1:
                 e, o = E - 1, PASSES - 1
                 interleave(nc.vector.tensor_copy, e, o, 0, P)
                 for b in range(BLOCKS + 1):
@@ -151,7 +162,7 @@ def tile_moe_res_lin_none_kernel(tc, x_words, x_scales, xr, w, gate, offs, out):
                         quantise(e, o, b * P, (b + 1) * P)
                         multiply(e, o, b)
                     if b > 0:
-                        scatter(q, b - 1)
+                        scatter(e, b - 1)
 
         for b in range(BLOCKS):
             cuts = (0, HALF, T) if b < BLOCKS - 1 else (0, HALF, T - HALF // 2, T)

@@ -32,6 +32,9 @@ RUN = 4
 DEPTH = 2
 GATE_ROW = SLOTS // P
 BANK = 512
+GROUP_ENDS = ((2, 4, 7, 8), (2, 5, 8))
+ON_SCALAR = (2, 4, 5, 7)
+ON_GPSIMD = (2, 5, 7)
 HALF = T // 2
 
 
@@ -61,10 +64,11 @@ def tile_moe_res_lin_none_kernel(tc, x_words, x_scales, xr, w, gate, offs, out):
             nc.sync.dma_start(out=token_words[o][:], in_=x_words[o].rearrange("p t r -> p (t r)").bitcast(I32))
 
         nc.gpsimd.memset(token_scales[:].bitcast(I32), 0)
-        nc.sync.dma_start(offsets[:], offs)
-        nc.sync.dma_start(out=gate_row[:], in_=gate[0, :].rearrange("(p i) -> p i", i=GATE_ROW))
         for o in range(PASSES):
             load_x(o)
+            if o == 0:
+                nc.sync.dma_start(offsets[:], offs)
+                nc.sync.dma_start(out=gate_row[:], in_=gate[0, :].rearrange("(p i) -> p i", i=GATE_ROW))
             for j in range(SCALE_ROWS):
                 nc.sync.dma_start(out=token_scales[SCALE_ROWS * o + j:P:QUADRANT, :].bitcast(I32),
                                   in_=x_scales[o, j::SCALE_ROWS, :].bitcast(I32))
@@ -95,18 +99,28 @@ def tile_moe_res_lin_none_kernel(tc, x_words, x_scales, xr, w, gate, offs, out):
             if o == PASSES - 1:
                 nc.vector.tensor_copy(slot_scales[:], token_scales[:].indirect(offsets[:]))
 
+        def rounded(e, o, lo, hi):
+            if e in ON_GPSIMD and (o, lo) == (0, 2 * P):
+                return before[:, lo * PACK:hi * PACK]
+            return made[e % 2, o][0][:, lo * PACK:hi * PACK]
+
         def interleave(copy, e, o, lo, hi):
-            copy(out=made[e % 2, o][0][:, lo * PACK:hi * PACK].rearrange("p (c i t) -> p c t i", i=RUN, t=PACK),
+            copy(out=rounded(e, o, lo, hi).rearrange("p (c i t) -> p c t i", i=RUN, t=PACK),
                  in_=raw[e][o][:, :, lo:hi].rearrange("p t (c i) -> p c t i", i=RUN))
 
+        def interleave_on_gpsimd(e, o, lo, hi):
+            nc.gpsimd.tensor_scalar(out=rounded(e, o, lo, hi).rearrange("p (n t) -> p n t", t=PACK),
+                                    in0=raw[e][o][:, :, lo:hi].rearrange("p t n -> p n t"),
+                                    scalar1=1.0, scalar2=0.0, op0=MULT, op1=ADD)
+
         def quantise(e, o, lo, hi):
-            rounded, codes, scales = made[e % 2, o]
-            nc.vector.quantize_mx(out=codes[:, lo:hi].bitcast(FP8X4), scales=scales[:, lo:hi], in_=rounded[:, lo * PACK:hi * PACK])
+            codes, scales = made[e % 2, o][1:]
+            nc.vector.quantize_mx(out=codes[:, lo:hi].bitcast(FP8X4), scales=scales[:, lo:hi], in_=rounded(e, o, lo, hi))
 
         def group(e, b):
-            if b == 0 and e >= E - 4:
-                return (E - 4, E - 1) if e < E - 1 else (E - 1, E)
-            return (e - e % 2, e - e % 2 + 2)
+            ends = GROUP_ENDS[min(b, 1)]
+            i = min(i for i in range(len(ends)) if e < ends[i])
+            return (ends[i - 1] if i > 0 else 0, ends[i])
 
         def multiply(e, o, b):
             codes, scales = made[e % 2, o][1:]
@@ -121,16 +135,23 @@ def tile_moe_res_lin_none_kernel(tc, x_words, x_scales, xr, w, gate, offs, out):
 
         def scatter(e, b):
             first, end = group(e, b)
-            if e < end - 1:
+            early = b > 0 and e == E - 2
+            if e < end - 1 and not early:
+                return
+            lo = E - 1 if b > 0 and e == E - 1 else first
+            if lo == first:
+                gated[b] = ring.tile([P, (end - first) * C], F32, name="gated%d" % b)
+            cols = slice((lo - first) * C, (e + 1 - first) * C)
+            nc.vector.tensor_tensor(gated[b][:, cols], acc[b][:, cols], gates[:, lo * C:(e + 1) * C], MULT)
+            if early:
                 return
             window = routed[b][:].indirect(offsets[:, first * C // LIST_ROWS:end * C // LIST_ROWS])
-            gated = ring.tile([P, (end - first) * C], F32, name="gated%d" % b)
-            nc.vector.tensor_tensor(gated[:], acc[b][:], gates[:, first * C:end * C], MULT)
             if end - first == 1:
-                nc.vector.tensor_tensor(window, gated[:], zeros[:], ADD)
+                nc.vector.tensor_tensor(window, gated[b][:], zeros[:], ADD)
             else:
-                nc.scalar.activation(out=window, in_=gated[:], func=COPY)
+                nc.scalar.activation(out=window, in_=gated[b][:], func=COPY)
 
+        gated = {}
         acc = {}
         for q in range(PAIRS):
             made = {(side, o): (ring.tile([P, N * PACK], BF16, name="rounded%d_%d" % (side, o), align_bytes=64),
@@ -142,9 +163,12 @@ def tile_moe_res_lin_none_kernel(tc, x_words, x_scales, xr, w, gate, offs, out):
                     if (e, o) == (E - 1, PASSES - 1):
                         continue
                     cuts = ((0, 2 * P), (2 * P, N))
-                    on_scalar = cuts if q == 0 and (e, o) != (1, 1) else cuts[:1] if (e % 2, o) == (0, 0) else ()
+                    on_scalar = cuts if q == 0 and (e, o) != (1, 1) else cuts[:1] if e in ON_SCALAR and o == 0 else ()
                     for cut in cuts:
-                        interleave(nc.scalar.copy if cut in on_scalar else nc.vector.tensor_copy, e, o, *cut)
+                        if e in ON_GPSIMD and o == 0 and cut not in on_scalar:
+                            interleave_on_gpsimd(e, o, *cut)
+                        else:
+                            interleave(nc.scalar.copy if cut in on_scalar else nc.vector.tensor_copy, e, o, *cut)
                     for cut in cuts:
                         quantise(e, o, *cut)
                     for b in range(BLOCKS):
@@ -152,6 +176,7 @@ def tile_moe_res_lin_none_kernel(tc, x_words, x_scales, xr, w, gate, offs, out):
                     if o == PASSES - 1:
                         for b in range(BLOCKS):
                             scatter(e, b)
+                        before = made[e % 2, o][0]
             if q == PAIRS - 1:
                 e, o = E - 1, PASSES - 1
                 interleave(nc.vector.tensor_copy, e, o, 0, P)

@@ -69,9 +69,10 @@ def tile_moe_res_lin_none_kernel(tc, x_words, x_scales, xr, w, gate, offs, out):
             if o == 0:
                 nc.sync.dma_start(offsets[:], offs)
                 nc.sync.dma_start(out=gate_row[:], in_=gate[0, :].rearrange("(p i) -> p i", i=GATE_ROW))
-            for j in range(SCALE_ROWS):
-                nc.sync.dma_start(out=token_scales[SCALE_ROWS * o + j:P:QUADRANT, :].bitcast(I32),
-                                  in_=x_scales[o, j::SCALE_ROWS, :].bitcast(I32))
+            for j in range(o * SCALE_ROWS // PASSES, (o + 1) * SCALE_ROWS // PASSES):
+                for u in range(PASSES):
+                    nc.sync.dma_start(out=token_scales[SCALE_ROWS * u + j:P:QUADRANT, :].bitcast(I32),
+                                      in_=x_scales[u, j::SCALE_ROWS, :].bitcast(I32))
         for e in range(E):
             for o in range(PASSES):
                 load_w(e, o)

@@ -35,7 +35,7 @@ BANK = 512
 GROUP_ENDS = ((2, 4, 7, 8), (2, 5, 8))
 ON_SCALAR = (2, 4, 5, 7)
 ON_GPSIMD = (2, 5, 7)
-HALF = T // 2
+STORE_CUTS = (0, 640, 1344, T)
 
 
 def tile_moe_res_lin_none_kernel(tc, x_words, x_scales, xr, w, gate, offs, out):
@@ -191,8 +191,7 @@ def tile_moe_res_lin_none_kernel(tc, x_words, x_scales, xr, w, gate, offs, out):
                         scatter(e, b - 1)
 
         for b in range(BLOCKS):
-            cuts = (0, HALF, T) if b < BLOCKS - 1 else (0, HALF, T - HALF // 2, T)
-            for lo, hi in zip(cuts, cuts[1:]):
+            for lo, hi in zip(STORE_CUTS, STORE_CUTS[1:]):
                 tokens = slice(lo, hi)
                 nc.vector.tensor_tensor(resid[b][:, tokens], resid[b][:, tokens], routed[b][:, tokens], ADD)
                 nc.sync.dma_start(out=out[b * P:(b + 1) * P, tokens], in_=resid[b][:, tokens])

@@ -30,12 +30,11 @@ QUADRANT = 32
 SCALE_ROWS = 4
 RUN = 4
 DEPTH = 2
-GATE_ROW = SLOTS // P
 BANK = 512
 GROUP_ENDS = ((2, 4, 7, 8), (2, 5, 8))
 ON_SCALAR = (2, 4, 5, 7)
 ON_GPSIMD = (2, 5, 7)
-STORE_CUTS = (0, 640, 1344, T)
+FIRST_CUTS = (0, 640, 1344, T)
 
 
 def tile_moe_res_lin_none_kernel(tc, x_words, x_scales, xr, w, gate, offs, out):
@@ -50,7 +49,8 @@ def tile_moe_res_lin_none_kernel(tc, x_words, x_scales, xr, w, gate, offs, out):
         token_words = [keep.tile([P, T], I32, name="token_words%d" % o) for o in range(PASSES)]
         slot_words = [keep.tile([P, SLOTS], U32, name="slot_words%d" % o, align_bytes=64) for o in range(PASSES)]
         slot_scales = keep.tile([P, SLOTS], U8, name="slot_scales", align_bytes=64)
-        gate_row = keep.tile([P, GATE_ROW], F32, name="gate_row")
+        gate_rows = keep.tile([P, C], F32, name="gate_rows")
+        gate_cols = keep.tile([P, E], F32, name="gate_cols")
         gates = keep.tile([P, SLOTS], F32, name="gates")
         identity = keep.tile([P, P], F32, name="identity")
         routed = [keep.tile([P, T], F32, name="routed%d" % b) for b in range(BLOCKS)]
@@ -63,12 +63,13 @@ def tile_moe_res_lin_none_kernel(tc, x_words, x_scales, xr, w, gate, offs, out):
         def load_x(o):
             nc.sync.dma_start(out=token_words[o][:], in_=x_words[o].rearrange("p t r -> p (t r)").bitcast(I32))
 
+        nc.gpsimd.memset(gate_rows[:], 0.0)
         nc.gpsimd.memset(token_scales[:].bitcast(I32), 0)
         for o in range(PASSES):
             load_x(o)
             if o == 0:
                 nc.sync.dma_start(offsets[:], offs)
-                nc.sync.dma_start(out=gate_row[:], in_=gate[0, :].rearrange("(p i) -> p i", i=GATE_ROW))
+                nc.sync.dma_start(out=gate_rows[0:E, :], in_=gate[0, :].rearrange("(e c) -> e c", c=C))
             for j in range(o * SCALE_ROWS // PASSES, (o + 1) * SCALE_ROWS // PASSES):
                 for u in range(PASSES):
                     nc.sync.dma_start(out=token_scales[SCALE_ROWS * u + j:P:QUADRANT, :].bitcast(I32),
@@ -87,13 +88,15 @@ def tile_moe_res_lin_none_kernel(tc, x_words, x_scales, xr, w, gate, offs, out):
 
         make_identity(nc, identity[:])
         per_bank = BANK // P
-        for h in range(GATE_ROW // per_bank):
-            spread = psum.tile([P, per_bank, P], F32, name="spread")
+        turned = psum.tile([P, P], F32, name="acc0")
+        nc.tensor.transpose(turned[:], gate_rows[:], identity[:])
+        nc.scalar.copy(out=gate_cols[:], in_=turned[:, 0:E])
+        for h in range(E // per_bank):
+            spread = psum.tile([P, per_bank, C], F32, name="spread")
             for i in range(per_bank):
-                column = h * per_bank + i
-                nc.tensor.transpose(spread[:, i, :], gate_row[:, column:column + 1].to_broadcast([P, P]), identity[:])
-            nc.scalar.copy(out=gates[:].rearrange("p (s i) -> p s i", i=GATE_ROW)[:, :, h * per_bank:(h + 1) * per_bank],
-                           in_=spread[:].rearrange("p i s -> p s i"))
+                e = h * per_bank + i
+                nc.tensor.transpose(spread[:, i, :], gate_cols[:, e:e + 1].to_broadcast([P, P]), identity[:])
+            nc.scalar.copy(out=gates[:, h * BANK:(h + 1) * BANK], in_=spread[:].rearrange("p i c -> p (i c)"))
 
         for o in range(PASSES):
             nc.vector.tensor_copy(slot_words[o][:], token_words[o][:].bitcast(U32).indirect(offsets[:]))
@@ -191,7 +194,8 @@ def tile_moe_res_lin_none_kernel(tc, x_words, x_scales, xr, w, gate, offs, out):
                         scatter(e, b - 1)
 
         for b in range(BLOCKS):
-            for lo, hi in zip(STORE_CUTS, STORE_CUTS[1:]):
+            cuts = FIRST_CUTS if b == 0 else (0, T // 2, T)
+            for lo, hi in zip(cuts, cuts[1:]):
                 tokens = slice(lo, hi)
                 nc.vector.tensor_tensor(resid[b][:, tokens], resid[b][:, tokens], routed[b][:, tokens], ADD)
                 nc.sync.dma_start(out=out[b * P:(b + 1) * P, tokens], in_=resid[b][:, tokens])

@@ -33,7 +33,8 @@ DEPTH = 2
 BANK = 512
 GROUP_ENDS = ((2, 4, 7, 8), (2, 5, 8))
 ON_SCALAR = (2, 4, 5, 7)
-ON_GPSIMD = (2, 5, 7)
+EACH_FROM = 5
+ON_GPSIMD = (2, 4, 5, 6, 7)
 FIRST_CUTS = (0, 640, 1344, T)
 
 
@@ -139,10 +140,10 @@ def tile_moe_res_lin_none_kernel(tc, x_words, x_scales, xr, w, gate, offs, out):
 
         def scatter(e, b):
             first, end = group(e, b)
-            early = b > 0 and e == E - 2
+            early = b > 0 and EACH_FROM <= e < end - 1
             if e < end - 1 and not early:
                 return
-            lo = E - 1 if b > 0 and e == E - 1 else first
+            lo = e if b > 0 and e > EACH_FROM else first
             if lo == first:
                 gated[b] = ring.tile([P, (end - first) * C], F32, name="gated%d" % b)
             cols = slice((lo - first) * C, (e + 1 - first) * C)
@@ -169,7 +170,7 @@ def tile_moe_res_lin_none_kernel(tc, x_words, x_scales, xr, w, gate, offs, out):
                     cuts = ((0, 2 * P), (2 * P, N))
                     on_scalar = cuts if q == 0 and (e, o) != (1, 1) else cuts[:1] if e in ON_SCALAR and o == 0 else ()
                     for cut in cuts:
-                        if e in ON_GPSIMD and o == 0 and cut not in on_scalar:
+                        if e in ON_GPSIMD and o == 0 and cut == cuts[1]:
                             interleave_on_gpsimd(e, o, *cut)
                         else:
                             interleave(nc.scalar.copy if cut in on_scalar else nc.vector.tensor_copy, e, o, *cut)
@@ -178,7 +179,7 @@ def tile_moe_res_lin_none_kernel(tc, x_words, x_scales, xr, w, gate, offs, out):
                     for b in range(BLOCKS):
                         multiply(e, o, b)
                     if o == PASSES - 1:
-                        for b in range(BLOCKS):
+                        for b in range(BLOCKS) if e < E - 2 else reversed(range(BLOCKS)):
                             scatter(e, b)
                         before = made[e % 2, o][0]
             if q == PAIRS - 1:

@@ -30,6 +30,7 @@ QUADRANT = 32
 SCALE_ROWS = 4
 RUN = 4
 DEPTH = 2
+BURST = 256
 BANK = 512
 GROUP_ENDS = ((2, 4, 7, 8), (2, 5, 8))
 ON_SCALAR = (2, 4, 5, 7)
@@ -45,18 +46,18 @@ def tile_moe_res_lin_none_kernel(tc, x_words, x_scales, xr, w, gate, offs, out):
         ring = ctx.enter_context(tc.tile_pool(name="ring", bufs=DEPTH))
         psum = ctx.enter_context(tc.psum_pool(name="psum", bufs=DEPTH))
 
-        offsets = keep.tile([P, SLOTS // LIST_ROWS], U16, name="offsets")
-        token_scales = keep.tile([P, T], U8, name="token_scales")
-        token_words = [keep.tile([P, T], I32, name="token_words%d" % o) for o in range(PASSES)]
+        offsets = keep.tile([P, SLOTS // LIST_ROWS], U16, name="offsets", align_bytes=BURST)
+        token_scales = keep.tile([P, T], U8, name="token_scales", align_bytes=BURST)
+        token_words = [keep.tile([P, T], I32, name="token_words%d" % o, align_bytes=BURST) for o in range(PASSES)]
         slot_words = [keep.tile([P, SLOTS], U32, name="slot_words%d" % o, align_bytes=64) for o in range(PASSES)]
         slot_scales = keep.tile([P, SLOTS], U8, name="slot_scales", align_bytes=64)
-        gate_rows = keep.tile([P, C], F32, name="gate_rows")
+        gate_rows = keep.tile([P, C], F32, name="gate_rows", align_bytes=BURST)
         gate_cols = keep.tile([P, E], F32, name="gate_cols")
         gates = keep.tile([P, SLOTS], F32, name="gates")
         identity = keep.tile([P, P], F32, name="identity")
         routed = [keep.tile([P, T], F32, name="routed%d" % b) for b in range(BLOCKS)]
-        resid = [keep.tile([P, T], F32, name="resid%d" % b) for b in range(BLOCKS)]
-        raw = [[keep.tile([P, PACK, N], F32, name="raw%d_%d" % (e, o)) for o in range(PASSES)] for e in range(E)]
+        resid = [keep.tile([P, T], F32, name="resid%d" % b, align_bytes=BURST) for b in range(BLOCKS)]
+        raw = [[keep.tile([P, PACK, N], F32, name="raw%d_%d" % (e, o), align_bytes=BURST) for o in range(PASSES)] for e in range(E)]
 
         def load_w(e, o):
             nc.sync.dma_start(out=raw[e][o][:], in_=w[e, o * K_PASS:(o + 1) * K_PASS, :].rearrange("(p t) n -> p t n", t=PACK))

@@ -36,7 +36,7 @@ GROUP_ENDS = ((2, 4, 7, 8), (2, 5, 8))
 ON_SCALAR = (2, 4, 5, 7)
 EACH_FROM = 5
 ON_GPSIMD = (2, 4, 5, 6, 7)
-FIRST_CUTS = (0, 640, 1344, T)
+STORE_CUTS = (0, 640, 1280, T)
 
 
 def tile_moe_res_lin_none_kernel(tc, x_words, x_scales, xr, w, gate, offs, out):
@@ -196,8 +196,7 @@ def tile_moe_res_lin_none_kernel(tc, x_words, x_scales, xr, w, gate, offs, out):
                         scatter(e, b - 1)
 
         for b in range(BLOCKS):
-            cuts = FIRST_CUTS if b == 0 else (0, T // 2, T)
-            for lo, hi in zip(cuts, cuts[1:]):
+            for lo, hi in zip(STORE_CUTS, STORE_CUTS[1:]):
                 tokens = slice(lo, hi)
                 nc.vector.tensor_tensor(resid[b][:, tokens], resid[b][:, tokens], routed[b][:, tokens], ADD)
                 nc.sync.dma_start(out=out[b * P:(b + 1) * P, tokens], in_=resid[b][:, tokens])

@@ -28,7 +28,7 @@ PAIR = 2 * C
 LIST_ROWS = 16
 QUADRANT = 32
 SCALE_ROWS = 4
-RUN = 4
+RUN = 2
 DEPTH = 2
 BURST = 256
 BANK = 512

@@ -36,7 +36,7 @@ GROUP_ENDS = ((2, 4, 7, 8), (2, 5, 8))
 ON_SCALAR = (2, 4, 5, 7)
 EACH_FROM = 5
 ON_GPSIMD = (2, 4, 5, 6, 7)
-STORE_CUTS = (0, 640, 1280, T)
+STORE_CUTS = (0, 640, 1344, T)
 
 
 def tile_moe_res_lin_none_kernel(tc, x_words, x_scales, xr, w, gate, offs, out):
@@ -57,10 +57,12 @@ def tile_moe_res_lin_none_kernel(tc, x_words, x_scales, xr, w, gate, offs, out):
         identity = keep.tile([P, P], F32, name="identity")
         routed = [keep.tile([P, T], F32, name="routed%d" % b) for b in range(BLOCKS)]
         resid = [keep.tile([P, T], F32, name="resid%d" % b, align_bytes=BURST) for b in range(BLOCKS)]
-        raw = [[keep.tile([P, PACK, N], F32, name="raw%d_%d" % (e, o), align_bytes=BURST) for o in range(PASSES)] for e in range(E)]
+        first_expert = keep.tile([P, PASSES, PACK, N], F32, name="first_expert", align_bytes=BURST)
+        raw = [[first_expert[:, o] if e == 0 else keep.tile([P, PACK, N], F32, name="raw%d_%d" % (e, o), align_bytes=BURST)[:]
+                for o in range(PASSES)] for e in range(E)]
 
         def load_w(e, o):
-            nc.sync.dma_start(out=raw[e][o][:], in_=w[e, o * K_PASS:(o + 1) * K_PASS, :].rearrange("(p t) n -> p t n", t=PACK))
+            nc.sync.dma_start(out=raw[e][o], in_=w[e, o * K_PASS:(o + 1) * K_PASS, :].rearrange("(p t) n -> p t n", t=PACK))
 
         def load_x(o):
             nc.sync.dma_start(out=token_words[o][:], in_=x_words[o].rearrange("p t r -> p (t r)").bitcast(I32))
@@ -76,7 +78,9 @@ def tile_moe_res_lin_none_kernel(tc, x_words, x_scales, xr, w, gate, offs, out):
                 for u in range(PASSES):
                     nc.sync.dma_start(out=token_scales[SCALE_ROWS * u + j:P:QUADRANT, :].bitcast(I32),
                                       in_=x_scales[u, j::SCALE_ROWS, :].bitcast(I32))
-        for e in range(E):
+        nc.sync.dma_start(out=first_expert[:].rearrange("p o t n -> p o (t n)"),
+                          in_=w[0].rearrange("(o p t) n -> p o (t n)", p=P, t=PACK))
+        for e in range(1, E):
             for o in range(PASSES):
                 load_w(e, o)
         for b in range(BLOCKS):
@@ -169,7 +173,7 @@ def tile_moe_res_lin_none_kernel(tc, x_words, x_scales, xr, w, gate, offs, out):
                     if (e, o) == (E - 1, PASSES - 1):
                         continue
                     cuts = ((0, 2 * P), (2 * P, N))
-                    on_scalar = cuts if q == 0 and (e, o) != (1, 1) else cuts[:1] if e in ON_SCALAR and o == 0 else ()
+                    on_scalar = cuts if e == 0 else cuts[1:] if (e, o) == (1, 1) else cuts[:1] if e in ON_SCALAR and o == 0 else ()
                     for cut in cuts:
                         if e in ON_GPSIMD and o == 0 and cut == cuts[1]:
                             interleave_on_gpsimd(e, o, *cut)

from contextlib import ExitStack

import concourse.mybir as mybir
from concourse.masks import make_identity

K, T, E, C, N = 1024, 2048, 8, 128, 384
FLOPS = 2 * K * N * E * C

F32 = mybir.dt.float32
BF16 = mybir.dt.bfloat16
I32 = mybir.dt.int32
U32 = mybir.dt.uint32
U16 = mybir.dt.uint16
U8 = mybir.dt.uint8
FP8X4 = mybir.dt.float8_e4m3fn_x4
MULT = mybir.AluOpType.mult
ADD = mybir.AluOpType.add
COPY = mybir.ActivationFunctionType.Copy

P = 128
PACK = 4
K_PASS = P * PACK
PASSES = K // K_PASS
BLOCKS = N // P
SLOTS = E * C
PAIRS = E // 2
PAIR = 2 * C
LIST_ROWS = 16
QUADRANT = 32
SCALE_ROWS = 4
RUN = 2
DEPTH = 2
BURST = 256
BANK = 512
GROUP_ENDS = ((2, 4, 7, 8), (2, 5, 8))
ON_SCALAR = (2, 4, 5, 7)
EACH_FROM = 5
ON_GPSIMD = (2, 4, 5, 6, 7)
STORE_CUTS = (0, 640, 1344, T)


def tile_moe_res_lin_none_kernel(tc, x_words, x_scales, xr, w, gate, offs, out):
    nc = tc.nc
    with ExitStack() as ctx:
        keep = ctx.enter_context(tc.tile_pool(name="keep", bufs=1))
        ring = ctx.enter_context(tc.tile_pool(name="ring", bufs=DEPTH))
        psum = ctx.enter_context(tc.psum_pool(name="psum", bufs=DEPTH))

        offsets = keep.tile([P, SLOTS // LIST_ROWS], U16, name="offsets", align_bytes=BURST)
        token_scales = keep.tile([P, T], U8, name="token_scales", align_bytes=BURST)
        token_words = [keep.tile([P, T], I32, name="token_words%d" % o, align_bytes=BURST) for o in range(PASSES)]
        slot_words = [keep.tile([P, SLOTS], U32, name="slot_words%d" % o, align_bytes=64) for o in range(PASSES)]
        slot_scales = keep.tile([P, SLOTS], U8, name="slot_scales", align_bytes=64)
        gate_rows = keep.tile([P, C], F32, name="gate_rows", align_bytes=BURST)
        gate_cols = keep.tile([P, E], F32, name="gate_cols")
        gates = keep.tile([P, SLOTS], F32, name="gates")
        identity = keep.tile([P, P], F32, name="identity")
        routed = [keep.tile([P, T], F32, name="routed%d" % b) for b in range(BLOCKS)]
        resid = [keep.tile([P, T], F32, name="resid%d" % b, align_bytes=BURST) for b in range(BLOCKS)]
        first_expert = keep.tile([P, PASSES, PACK, N], F32, name="first_expert", align_bytes=BURST)
        raw = [[first_expert[:, o] if e == 0 else keep.tile([P, PACK, N], F32, name="raw%d_%d" % (e, o), align_bytes=BURST)[:]
                for o in range(PASSES)] for e in range(E)]

        def load_w(e, o):
            nc.sync.dma_start(out=raw[e][o], in_=w[e, o * K_PASS:(o + 1) * K_PASS, :].rearrange("(p t) n -> p t n", t=PACK))

        def load_x(o):
            nc.sync.dma_start(out=token_words[o][:], in_=x_words[o].rearrange("p t r -> p (t r)").bitcast(I32))

        nc.gpsimd.memset(gate_rows[:], 0.0)
        nc.gpsimd.memset(token_scales[:].bitcast(I32), 0)
        for o in range(PASSES):
            load_x(o)
            if o == 0:
                nc.sync.dma_start(offsets[:], offs)
                nc.sync.dma_start(out=gate_rows[0:E, :], in_=gate[0, :].rearrange("(e c) -> e c", c=C))
            for j in range(o * SCALE_ROWS // PASSES, (o + 1) * SCALE_ROWS // PASSES):
                for u in range(PASSES):
                    nc.sync.dma_start(out=token_scales[SCALE_ROWS * u + j:P:QUADRANT, :].bitcast(I32),
                                      in_=x_scales[u, j::SCALE_ROWS, :].bitcast(I32))
        nc.sync.dma_start(out=first_expert[:].rearrange("p o t n -> p o (t n)"),
                          in_=w[0].rearrange("(o p t) n -> p o (t n)", p=P, t=PACK))
        for e in range(1, E):
            for o in range(PASSES):
                load_w(e, o)
        for b in range(BLOCKS):
            nc.sync.dma_start(out=resid[b][:], in_=xr[b * P:(b + 1) * P, :])

        zeros = keep.tile([P, P], F32, name="zeros")
        nc.vector.memset(zeros[:], 0.0)
        for b in range(BLOCKS):
            copy = nc.vector.tensor_copy if b == 0 else nc.scalar.copy
            copy(out=routed[b][:].rearrange("p (r c) -> p r c", c=P), in_=zeros[:].unsqueeze(1).to_broadcast([P, T // P, P]))

        make_identity(nc, identity[:])
        per_bank = BANK // P
        turned = psum.tile([P, P], F32, name="acc0")
        nc.tensor.transpose(turned[:], gate_rows[:], identity[:])
        nc.scalar.copy(out=gate_cols[:], in_=turned[:, 0:E])
        for h in range(E // per_bank):
            spread = psum.tile([P, per_bank, C], F32, name="spread")
            for i in range(per_bank):
                e = h * per_bank + i
                nc.tensor.transpose(spread[:, i, :], gate_cols[:, e:e + 1].to_broadcast([P, P]), identity[:])
            nc.scalar.copy(out=gates[:, h * BANK:(h + 1) * BANK], in_=spread[:].rearrange("p i c -> p (i c)"))

        for o in range(PASSES):
            nc.vector.tensor_copy(slot_words[o][:], token_words[o][:].bitcast(U32).indirect(offsets[:]))
            if o == PASSES - 1:
                nc.vector.tensor_copy(slot_scales[:], token_scales[:].indirect(offsets[:]))

        def rounded(e, o, lo, hi):
            if e in ON_GPSIMD and (o, lo) == (0, 2 * P):
                return before[:, lo * PACK:hi * PACK]
            return made[e % 2, o][0][:, lo * PACK:hi * PACK]

        def interleave(copy, e, o, lo, hi):
            copy(out=rounded(e, o, lo, hi).rearrange("p (c i t) -> p c t i", i=RUN, t=PACK),
                 in_=raw[e][o][:, :, lo:hi].rearrange("p t (c i) -> p c t i", i=RUN))

        def interleave_on_gpsimd(e, o, lo, hi):
            nc.gpsimd.tensor_scalar(out=rounded(e, o, lo, hi).rearrange("p (n t) -> p n t", t=PACK),
                                    in0=raw[e][o][:, :, lo:hi].rearrange("p t n -> p n t"),
                                    scalar1=1.0, scalar2=0.0, op0=MULT, op1=ADD)

        def quantise(e, o, lo, hi):
            codes, scales = made[e % 2, o][1:]
            nc.vector.quantize_mx(out=codes[:, lo:hi].bitcast(FP8X4), scales=scales[:, lo:hi], in_=rounded(e, o, lo, hi))

        def group(e, b):
            ends = GROUP_ENDS[min(b, 1)]
            i = min(i for i in range(len(ends)) if e < ends[i])
            return (ends[i - 1] if i > 0 else 0, ends[i])

        def multiply(e, o, b):
            codes, scales = made[e % 2, o][1:]
            first, end = group(e, b)
            if (e, o) == (first, 0):
                acc[b] = psum.tile([P, (end - first) * C], F32, name="acc%d" % b)
            cols, slots = slice(b * P, (b + 1) * P), slice(e * C, (e + 1) * C)
            nc.tensor.matmul_mx(out=acc[b][:, (e - first) * C:(e - first + 1) * C],
                                lhsT=codes[:, cols].bitcast(FP8X4), lhsT_scale=scales[:, cols],
                                rhs=slot_words[o][:, slots].bitcast(FP8X4), rhs_scale=slot_scales[SCALE_ROWS * o:P, slots],
                                start=(o == 0), stop=(o == PASSES - 1))

        def scatter(e, b):
            first, end = group(e, b)
            early = b > 0 and EACH_FROM <= e < end - 1
            if e < end - 1 and not early:
                return
            lo = e if b > 0 and e > EACH_FROM else first
            if lo == first:
                gated[b] = ring.tile([P, (end - first) * C], F32, name="gated%d" % b)
            cols = slice((lo - first) * C, (e + 1 - first) * C)
            nc.vector.tensor_tensor(gated[b][:, cols], acc[b][:, cols], gates[:, lo * C:(e + 1) * C], MULT)
            if early:
                return
            window = routed[b][:].indirect(offsets[:, first * C // LIST_ROWS:end * C // LIST_ROWS])
            if end - first == 1:
                nc.vector.tensor_tensor(window, gated[b][:], zeros[:], ADD)
            else:
                nc.scalar.activation(out=window, in_=gated[b][:], func=COPY)

        gated = {}
        acc = {}
        for q in range(PAIRS):
            made = {(side, o): (ring.tile([P, N * PACK], BF16, name="rounded%d_%d" % (side, o), align_bytes=64),
                                ring.tile([P, N], U32, name="codes%d_%d" % (side, o), align_bytes=64),
                                ring.tile([P, N], U8, name="scales%d_%d" % (side, o), align_bytes=64))
                    for side in range(2) for o in range(PASSES)}
            for e in (2 * q, 2 * q + 1):
                for o in range(PASSES):
                    if (e, o) == (E - 1, PASSES - 1):
                        continue
                    cuts = ((0, 2 * P), (2 * P, N))
                    on_scalar = cuts if e == 0 else cuts[1:] if (e, o) == (1, 1) else cuts[:1] if e in ON_SCALAR and o == 0 else ()
                    for cut in cuts:
                        if e in ON_GPSIMD and o == 0 and cut == cuts[1]:
                            interleave_on_gpsimd(e, o, *cut)
                        else:
                            interleave(nc.scalar.copy if cut in on_scalar else nc.vector.tensor_copy, e, o, *cut)
                    for cut in cuts:
                        quantise(e, o, *cut)
                    for b in range(BLOCKS):
                        multiply(e, o, b)
                    if o == PASSES - 1:
                        for b in range(BLOCKS) if e < E - 2 else reversed(range(BLOCKS)):
                            scatter(e, b)
                        before = made[e % 2, o][0]
            if q == PAIRS - 1:
                e, o = E - 1, PASSES - 1
                interleave(nc.vector.tensor_copy, e, o, 0, P)
                for b in range(BLOCKS + 1):
                    if b + 1 < BLOCKS:
                        interleave(nc.vector.tensor_copy, e, o, (b + 1) * P, (b + 2) * P)
                    if b < BLOCKS:
                        quantise(e, o, b * P, (b + 1) * P)
                        multiply(e, o, b)
                    if b > 0:
                        scatter(e, b - 1)

        for b in range(BLOCKS):
            for lo, hi in zip(STORE_CUTS, STORE_CUTS[1:]):
                tokens = slice(lo, hi)
                nc.vector.tensor_tensor(resid[b][:, tokens], resid[b][:, tokens], routed[b][:, tokens], ADD)
                nc.sync.dma_start(out=out[b * P:(b + 1) * P, tokens], in_=resid[b][:, tokens])
